import numpy as np
import ml_dtypes


def mxq(x, axis, fmt="e4m3"):
    dtype, down = {"e4m3": (ml_dtypes.float8_e4m3fn, 7), "e5m2": (ml_dtypes.float8_e5m2, 14)}[fmt]
    v = np.moveaxis(np.asarray(x, np.float32).astype(ml_dtypes.bfloat16).astype(np.float64), axis, -1)
    blocks = v.reshape(v.shape[:-1] + (-1, 32))
    amax = np.abs(blocks).max(-1, keepdims=True)
    byte = np.maximum(np.where(amax > 0, np.frexp(amax)[1] - 1 + 127, 0) - down, 1)
    scale = np.exp2(byte - 127.0)
    codes = (blocks / scale).astype(np.float32).astype(dtype).astype(np.float64)
    return np.moveaxis((codes * scale).reshape(v.shape), -1, axis)


WIDE = False


def mx_kscale(k):
    if not WIDE:
        return np.ones(k)
    levels = np.array([10, -10, 5, -5, 0])
    if k % 512:
        return np.exp2(np.random.permutation(np.resize(levels, k // 32))).repeat(32)
    a = np.empty((k // 512, 16))
    for p in range(k // 512):
        a[p, :8] = np.random.permutation(np.resize(levels, 8))
        for g in range(8):
            far = levels[np.abs(levels - a[p, g]) >= 10]
            a[p, g + 8] = far[np.random.randint(len(far))]
    return np.exp2(a.ravel()).repeat(32)


def f64(x):
    return np.asarray(x).astype(np.float64)


def striped(idx):
    return np.tile(idx.reshape(-1, 16).T, (8, 1)).astype(np.uint16)


def unstriped(offs):
    return offs[:16].T.reshape(-1).astype(np.int64)


def pack_weight(w):
    k, n = w.shape
    w = f64(np.asarray(w, np.float32).astype(ml_dtypes.bfloat16)).reshape(k // 32, 32, n)
    amax = np.abs(w).max(1)
    byte = np.clip(np.where(amax > 0, np.frexp(amax)[1] - 1 + 127 - 7, 1), 1, 254)
    scaled = (w * np.exp2(127.0 - byte)[:, None, :]).reshape(k, n).astype(np.float32)
    words = np.ascontiguousarray(scaled.reshape(k // 512, 128, 4, n).transpose(0, 1, 3, 2)).astype(ml_dtypes.float8_e4m3fn).view(np.uint8)
    return words, np.ascontiguousarray(byte.astype(np.uint8).reshape(k // 512, 16, n))


def unpack_weight(words, scales):
    g, p, n, _ = words.shape
    vals = np.ascontiguousarray(words).view(ml_dtypes.float8_e4m3fn).astype(np.float64) * np.repeat(np.exp2(scales.astype(np.float64) - 127.0), 8, axis=1)[..., None]
    return vals.transpose(0, 1, 3, 2).reshape(g * 512, n)


def sigmoid(v):
    return 1.0 / (1.0 + np.exp(-np.maximum(v, -700.0)))


K, T, S, H, D, V, W, U = 1024, 1024, 512, 512, 8, 128, 1024, 1024


def setup_inputs():
    n = np.random.standard_normal
    s = mx_kscale(K)[:, None]
    u = mx_kscale(H)
    packed_xT = pack_weight(n((K, T)) * s)
    packed_eT = pack_weight(n((H, W)) / np.sqrt(H) / u[:, None])
    return {
        "x_words": packed_xT[0],
        "x_scales": packed_xT[1],
        "w1": (n((K, H)) / np.sqrt(K) / s * u).astype(np.float32),
        "e_words": packed_eT[0],
        "e_scales": packed_eT[1],
        "pos": (n((S, V))).astype(np.float32),
        "offs": striped(np.random.permutation(T)[:S]),
        "neg": striped(np.random.permutation(W)[:U]),
    }


def reference(x_words, x_scales, w1, e_words, e_scales, pos, offs, neg):
    xq = unpack_weight(x_words, x_scales)[:, unstriped(offs)]
    h = mxq(f64(w1), 0, "e4m3").T @ xq
    e_neg = unpack_weight(e_words, e_scales)[:, unstriped(neg)]
    y = mxq(h, 0, "e4m3").T @ e_neg
    top = y.reshape(len(y), -1, D).max(axis=2)
    ex = np.exp(y - np.repeat(top, D, axis=1))
    total = ex.reshape(len(ex), -1, D).sum(axis=2)
    wgt = ex / np.repeat(total, D, axis=1)
    sp = np.repeat(f64(pos), D, axis=1)
    gg = sigmoid(y - sp)
    z = wgt * (gg + sigmoid((y) ** 2))
    return z.reshape(len(z), -1, D).sum(axis=2)

@@ -1,0 +1,229 @@
+from contextlib import ExitStack
+
+import concourse.mybir as mybir
+from concourse.masks import make_identity
+
+K, T, S, H, D, V, W, U = 1024, 1024, 512, 512, 8, 128, 1024, 1024
+FLOPS = 2 * K * H * S + 2 * H * S * U
+
+F32 = mybir.dt.float32
+BF16 = mybir.dt.bfloat16
+I32 = mybir.dt.int32
+U32 = mybir.dt.uint32
+U16 = mybir.dt.uint16
+U8 = mybir.dt.uint8
+FP8X4 = mybir.dt.float8_e4m3fn_x4
+ALU = mybir.AluOpType
+ACT = mybir.ActivationFunctionType
+
+P = 128
+PACK = 4
+PASSES = K // (P * PACK)
+BANK = 512
+GROUPS = BANK // D
+TILES = S // P
+M_SPLIT = 80
+TAIL = 32
+H_BANKS = ("total0", "total1", "num", "back")
+
+
+def tile_picked_ytop1_top1_p_kernel(tc, x_words, x_scales, w1, e_words, e_scales, pos, offs, neg, out):
+    nc = tc.nc
+    with ExitStack() as ctx:
+        keep = ctx.enter_context(tc.tile_pool(name="keep", bufs=1))
+        work = ctx.enter_context(tc.tile_pool(name="work", bufs=3))
+        psum = ctx.enter_context(tc.psum_pool(name="psum", bufs=1))
+
+        offs_sb = keep.tile([P, S // 16], U16, name="offs_sb")
+        neg_sb = keep.tile([P, U // 16], U16, name="neg_sb")
+        xw = [keep.tile([P, T], U32, name="xw%d" % g, align_bytes=64) for g in range(PASSES)]
+        xs = keep.tile([P, T], U8, name="xs", align_bytes=64)
+        ew = keep.tile([P, W], U32, name="ew", align_bytes=64)
+        es = keep.tile([P, W], U8, name="es", align_bytes=64)
+        w_raw = [keep.tile([P, PACK * H], F32, name="w_raw%d" % g, align_bytes=64) for g in range(PASSES)]
+        pos_sb = keep.tile([P, TILES, V], F32, name="pos_sb")
+        ident = keep.tile([P, P], F32, name="ident")
+
+        nc.gpsimd.memset(es[:].bitcast(I32), 0)
+        nc.gpsimd.memset(xs[:].bitcast(I32), 0)
+
+        def load_words(dst, words):
+            nc.sync.dma_start(dst[:].bitcast(I32), words.rearrange("p n t -> p (n t)").bitcast(I32))
+
+        def load_w1(g):
+            nc.sync.dma_start(w_raw[g][:], w1[512 * g : 512 * (g + 1), :].rearrange("(p j) c -> p (j c)", j=PACK))
+
+        nc.sync.dma_start(offs_sb[:], offs)
+        nc.sync.dma_start(neg_sb[:], neg)
+        for q in range(4):
+            nc.sync.dma_start(es[32 * q : 32 * q + 4, :].bitcast(I32), e_scales[0, 4 * q : 4 * q + 4, :].bitcast(I32))
+        load_w1(0)
+        load_words(xw[0], x_words[0])
+        for q in range(4):
+            nc.sync.dma_start(xs[32 * q : 32 * q + 4 * PASSES, :].bitcast(I32), x_scales[:, 4 * q : 4 * q + 4, :].bitcast(I32))
+        load_w1(1)
+        load_words(xw[1], x_words[1])
+        load_words(ew, e_words[0])
+        nc.sync.dma_start(pos_sb[:], pos.rearrange("(a p) v -> p a v", p=P))
+
+        make_identity(nc, ident[:])
+
+        xg = [keep.tile([P, S], U32, name="xg%d" % g, align_bytes=64) for g in range(PASSES)]
+        xsg = keep.tile([P, S], U8, name="xsg", align_bytes=64)
+        eg = [keep.tile([P, BANK], U32, name="eg0", align_bytes=64)]
+        esg = [keep.tile([P, BANK], U8, name="esg%d" % h, align_bytes=64) for h in range(U // BANK)]
+        wq = [keep.tile([P, H], U32, name="wq%d" % g, align_bytes=64) for g in range(PASSES)]
+        wsc = [keep.tile([P, H], U8, name="wsc%d" % g, align_bytes=64) for g in range(PASSES)]
+
+        def neg_cols(h):
+            return neg_sb[:, h * BANK // 16 : (h + 1) * BANK // 16]
+
+        def quantize_w1(g, m_split, pieces):
+            w_bf = keep.tile([P, PACK * H], BF16, name="w_bf%d" % g, align_bytes=64)
+            dst = w_bf[:].rearrange("p (t m j) -> p m t j", t=PACK, j=PACK)
+            src = w_raw[g][:].rearrange("p (j m t) -> p m t j", j=PACK, t=PACK)
+            nc.scalar.activation(dst[:, :m_split], src[:, :m_split], ACT.Copy)
+            if m_split < P:
+                nc.vector.tensor_copy(dst[:, m_split:], src[:, m_split:])
+            n = H // pieces
+            for c in range(pieces):
+                cols = slice(n * c, n * (c + 1))
+                nc.vector.quantize_mx(out=wq[g][:, cols].bitcast(FP8X4), scales=wsc[g][:, cols], in_=w_bf[:, PACK * n * c : PACK * n * (c + 1)])
+
+        for h in range(U // BANK):
+            nc.vector.tensor_copy(esg[h][:], es[:].indirect(neg_cols(h)))
+        nc.vector.tensor_copy(xg[0][:], xw[0][:].indirect(offs_sb[:]))
+        nc.vector.tensor_copy(xsg[:], xs[:].indirect(offs_sb[:]))
+        quantize_w1(0, P, 1)
+        quantize_w1(1, M_SPLIT, 4)
+        nc.vector.tensor_copy(xg[1][:, :P], xw[1][:].indirect(offs_sb[:, : P // 16]))
+        nc.vector.tensor_copy(xg[1][:, P:], xw[1][:].indirect(offs_sb[:, P // 16 :]))
+        nc.vector.tensor_copy(eg[0][:], ew[:].indirect(neg_cols(0)))
+
+        def hidden(i):
+            tok = slice(P * i, P * (i + 1))
+            h_ps = psum.tile([P, PACK, P], F32, name="h_ps", tag=H_BANKS[i])
+            for j in range(PACK):
+                for g in range(PASSES):
+                    nc.tensor.matmul_mx(
+                        out=h_ps[:, j, :],
+                        lhsT=wq[g][:, P * j : P * (j + 1)].bitcast(FP8X4),
+                        lhsT_scale=wsc[g][:, P * j : P * (j + 1)],
+                        rhs=xg[g][:, tok].bitcast(FP8X4),
+                        rhs_scale=xsg[4 * g : P, tok],
+                        start=(g == 0),
+                        stop=(g == PASSES - 1),
+                    )
+            h_bf = keep.tile([P, P * PACK], BF16, name="h_bf", tag="h_bf%d" % i, align_bytes=64)
+            nc.scalar.activation(h_bf[:].rearrange("p (n j) -> p n j", j=PACK), h_ps[:].rearrange("p j n -> p n j"), ACT.Copy)
+            hq = keep.tile([P, P], U32, name="hq%d" % i, align_bytes=64)
+            hs = keep.tile([P, P], U8, name="hs%d" % i, align_bytes=64)
+            nc.vector.quantize_mx(out=hq[:].bitcast(FP8X4), scales=hs[:], in_=h_bf[:])
+            return hq, hs
+
+        def scores(hq, hs):
+            banks = []
+            for h in range(U // BANK):
+                y_ps = psum.tile([P, BANK], F32, name="y_ps", bufs=4)
+                nc.tensor.matmul_mx(
+                    out=y_ps[:], lhsT=hq[:].bitcast(FP8X4), lhsT_scale=hs[:],
+                    rhs=eg[h][:].bitcast(FP8X4), rhs_scale=esg[h][:], start=True, stop=True,
+                )
+                banks.append(y_ps)
+            return banks
+
+        def sum_over_group(acc, terms):
+            for d in range(D):
+                nc.tensor.matmul(acc, lhsT=terms[:, d, :], rhs=ident[:], is_transpose=True, start=(d == 0), stop=(d == D - 1))
+
+        def loss(i, banks):
+            last = i + 1 == TILES
+            top = work.tile([P, V], F32, name="top")
+            below = work.tile([P, D, V], F32, name="below")
+            ex = work.tile([P, D, V], F32, name="ex")
+            args = work.tile([P, 2 * D, V], F32, name="args")
+            th = work.tile([P, 2 * D, V], F32, name="th")
+            both = work.tile([P, D, V], F32, name="both")
+            z = work.tile([P, D, V], F32, name="z")
+            wide = [P, D, GROUPS]
+            halves = [slice(GROUPS * h, GROUPS * (h + 1)) for h in range(len(banks))]
+
+            def y_dv(h):
+                return banks[h][:].rearrange("p (v d) -> p d v", d=D)
+
+            def gate_args(h):
+                vs = halves[h]
+                nc.vector.tensor_tensor(args[:, :D, vs], y_dv(h), pos_sb[:, i, vs].unsqueeze(1).to_broadcast(wide), ALU.subtract)
+                nc.scalar.activation(args[:, D:, vs], y_dv(h), ACT.Square)
+
+            def softmax_terms(h):
+                vs = halves[h]
+                nc.vector.tensor_reduce(top[:, vs], banks[h][:].rearrange("p (v d) -> p v d", d=D), mybir.AxisListType.X, ALU.max)
+                nc.vector.tensor_tensor(below[:, :, vs], y_dv(h), top[:, vs].unsqueeze(1).to_broadcast(wide), ALU.subtract)
+                nc.scalar.activation(ex[:, :, vs], below[:, :, vs], ACT.Exp)
+
+            def gates(vs):
+                nc.scalar.activation(th[:, :, vs], args[:, :, vs], ACT.Tanh, scale=0.5)
+
+            def inverse_total():
+                total = psum.tile([P, P], F32, name="total", tag=H_BANKS[i % 2])
+                sum_over_group(total[:], ex)
+                inv = work.tile([P, P], F32, name="inv")
+                nc.vector.reciprocal(inv[:], total[:])
+                return inv
+
+            if not last:
+                for h, vs in enumerate(halves):
+                    gate_args(h)
+                    gates(vs)
+                    softmax_terms(h)
+                    nc.gpsimd.tensor_tensor(both[:, :, vs], th[:, :D, vs], th[:, D:, vs], ALU.add)
+                    nc.gpsimd.tensor_tensor(z[:, :, vs], both[:, :, vs], ex[:, :, vs], ALU.mult)
+                inv = inverse_total()
+                num = psum.tile([P, P], F32, name="num")
+                sum_over_group(num[:], z)
+                ratio = work.tile([P, P], F32, name="ratio")
+                nc.vector.tensor_tensor(ratio[:], num[:], inv[:], ALU.mult)
+                back = psum.tile([P, P], F32, name="back")
+                nc.tensor.transpose(back[:], ratio[:], ident[:])
+                res = work.tile([P, V], F32, name="res")
+                nc.scalar.activation(res[:], back[:], ACT.Copy, bias=1.0, scale=0.5)
+                nc.sync.dma_start(out[P * i : P * (i + 1), :], res[:])
+                return
+
+            for h in range(len(banks)):
+                softmax_terms(h)
+            for h in range(len(banks)):
+                gate_args(h)
+            inv = inverse_total()
+            back = psum.tile([P, P], F32, name="back")
+            nc.tensor.transpose(back[:], inv[:], ident[:])
+            vs = halves[0]
+            gates(vs)
+            nc.gpsimd.tensor_tensor(both[:, :, vs], th[:, :D, vs], th[:, D:, vs], ALU.add)
+            nc.gpsimd.tensor_tensor(z[:, :, vs], both[:, :, vs], ex[:, :, vs], ALU.mult)
+            pieces = [slice(GROUPS + TAIL * c, GROUPS + TAIL * (c + 1)) for c in range(GROUPS // TAIL)]
+            for piece in pieces:
+                gates(piece)
+            num_sb = work.tile([P, V], F32, name="num_sb")
+            ratio = work.tile([P, GROUPS], F32, name="ratio_half")
+            res = work.tile([P, V], F32, name="res")
+            for piece in pieces:
+                nc.vector.tensor_tensor(both[:, :, piece], th[:, :D, piece], th[:, D:, piece], ALU.add)
+                nc.vector.scalar_tensor_tensor(z[:, :, piece], both[:, :, piece], 2.0, ex[:, :, piece], ALU.add, ALU.mult)
+                nc.vector.tensor_reduce(num_sb[:, piece], z[:, :, piece].rearrange("p d v -> p v d"), mybir.AxisListType.X, ALU.add)
+            nc.vector.scalar_tensor_tensor(res[:, halves[1]], num_sb[:, halves[1]], 0.5, back[:, halves[1]], ALU.mult, ALU.mult)
+            nc.vector.tensor_reduce(num_sb[:, vs], z[:, :, vs].rearrange("p d v -> p v d"), mybir.AxisListType.X, ALU.add)
+            nc.vector.tensor_tensor(ratio[:], num_sb[:, vs], back[:, vs], ALU.mult)
+            nc.scalar.activation(res[:, vs], ratio[:], ACT.Copy, bias=1.0, scale=0.5)
+            nc.sync.dma_start(out[P * i : P * (i + 1), :], res[:])
+
+        quantised = [hidden(0)]
+        eg.append(keep.tile([P, BANK], U32, name="eg1", tag="h_bf0", align_bytes=64))
+        quantised.extend(hidden(i) for i in range(1, TILES))
+        nc.vector.tensor_copy(eg[1][:], ew[:].indirect(neg_cols(1)))
+        banks = [scores(*quantised[0])]
+        for i in range(TILES):
+            if i + 1 < TILES:
+                banks.append(scores(*quantised[i + 1]))
+            loss(i, banks[i])

@@ -23,15 +23,18 @@ BANK = 512
 GROUPS = BANK // D
 TILES = S // P
 M_SPLIT = 80
+SQUARE_FIRST = 5
+LAST_PIECES = 4
 TAIL = 32
-H_BANKS = ("total0", "total1", "num", "back")
+H_BANKS = (0, 1, 3, 1)
+Y_BANKS = ((2, 3), (4, 5), (6, 7), (2, 3))
 
 
 def tile_picked_ytop1_top1_p_kernel(tc, x_words, x_scales, w1, e_words, e_scales, pos, offs, neg, out):
     nc = tc.nc
     with ExitStack() as ctx:
         keep = ctx.enter_context(tc.tile_pool(name="keep", bufs=1))
-        work = ctx.enter_context(tc.tile_pool(name="work", bufs=3))
+        work = ctx.enter_context(tc.tile_pool(name="work", bufs=4))
         psum = ctx.enter_context(tc.psum_pool(name="psum", bufs=1))
 
         offs_sb = keep.tile([P, S // 16], U16, name="offs_sb")
@@ -40,7 +43,7 @@ def tile_picked_ytop1_top1_p_kernel(tc, x_words, x_scales, w1, e_words, e_scales
         xs = keep.tile([P, T], U8, name="xs", align_bytes=64)
         ew = keep.tile([P, W], U32, name="ew", align_bytes=64)
         es = keep.tile([P, W], U8, name="es", align_bytes=64)
-        w_raw = [keep.tile([P, PACK * H], F32, name="w_raw%d" % g, align_bytes=64) for g in range(PASSES)]
+        w_raw = [keep.tile([P, PACK * H], F32, name="w_raw", tag="w_raw%d" % g, align_bytes=64) for g in range(PASSES)]
         pos_sb = keep.tile([P, TILES, V], F32, name="pos_sb")
         ident = keep.tile([P, P], F32, name="ident")
 
@@ -68,9 +71,10 @@ def tile_picked_ytop1_top1_p_kernel(tc, x_words, x_scales, w1, e_words, e_scales
 
         make_identity(nc, ident[:])
 
-        xg = [keep.tile([P, S], U32, name="xg%d" % g, align_bytes=64) for g in range(PASSES)]
+        xg0 = keep.tile([P, S], U32, name="xg0", align_bytes=64)
+        xg1_first = keep.tile([P, P], U32, name="xg1_first", align_bytes=64)
         xsg = keep.tile([P, S], U8, name="xsg", align_bytes=64)
-        eg = [keep.tile([P, BANK], U32, name="eg0", align_bytes=64)]
+        eg = [[keep.tile([P, BANK], U32, name="eg0", align_bytes=64)], []]
         esg = [keep.tile([P, BANK], U8, name="esg%d" % h, align_bytes=64) for h in range(U // BANK)]
         wq = [keep.tile([P, H], U32, name="wq%d" % g, align_bytes=64) for g in range(PASSES)]
         wsc = [keep.tile([P, H], U8, name="wsc%d" % g, align_bytes=64) for g in range(PASSES)]
@@ -79,7 +83,7 @@ def tile_picked_ytop1_top1_p_kernel(tc, x_words, x_scales, w1, e_words, e_scales
             return neg_sb[:, h * BANK // 16 : (h + 1) * BANK // 16]
 
         def quantize_w1(g, m_split, pieces):
-            w_bf = keep.tile([P, PACK * H], BF16, name="w_bf%d" % g, align_bytes=64)
+            w_bf = keep.tile([P, PACK * H], BF16, name="w_bf", tag="w_bf%d" % g, align_bytes=64)
             dst = w_bf[:].rearrange("p (t m j) -> p m t j", t=PACK, j=PACK)
             src = w_raw[g][:].rearrange("p (j m t) -> p m t j", j=PACK, t=PACK)
             nc.scalar.activation(dst[:, :m_split], src[:, :m_split], ACT.Copy)
@@ -92,24 +96,26 @@ def tile_picked_ytop1_top1_p_kernel(tc, x_words, x_scales, w1, e_words, e_scales
 
         for h in range(U // BANK):
             nc.vector.tensor_copy(esg[h][:], es[:].indirect(neg_cols(h)))
-        nc.vector.tensor_copy(xg[0][:], xw[0][:].indirect(offs_sb[:]))
+        nc.vector.tensor_copy(xg0[:], xw[0][:].indirect(offs_sb[:]))
         nc.vector.tensor_copy(xsg[:], xs[:].indirect(offs_sb[:]))
         quantize_w1(0, P, 1)
+        nc.vector.tensor_copy(xg1_first[:], xw[1][:].indirect(offs_sb[:, : P // 16]))
         quantize_w1(1, M_SPLIT, 4)
-        nc.vector.tensor_copy(xg[1][:, :P], xw[1][:].indirect(offs_sb[:, : P // 16]))
-        nc.vector.tensor_copy(xg[1][:, P:], xw[1][:].indirect(offs_sb[:, P // 16 :]))
-        nc.vector.tensor_copy(eg[0][:], ew[:].indirect(neg_cols(0)))
+        xg1_rest = keep.tile([P, S - P], U32, name="xg1_rest", tag="w_raw1", align_bytes=64)
+        nc.vector.tensor_copy(xg1_rest[:], xw[1][:].indirect(offs_sb[:, P // 16 :]))
+        nc.vector.tensor_copy(eg[0][0][:], ew[:].indirect(neg_cols(0)))
 
         def hidden(i):
             tok = slice(P * i, P * (i + 1))
-            h_ps = psum.tile([P, PACK, P], F32, name="h_ps", tag=H_BANKS[i])
+            x_codes = [xg0[:, tok], xg1_first[:] if i == 0 else xg1_rest[:, P * (i - 1) : P * i]]
+            h_ps = psum.tile([P, PACK, P], F32, name="h_ps", tag="bank%d" % H_BANKS[i])
             for j in range(PACK):
                 for g in range(PASSES):
                     nc.tensor.matmul_mx(
                         out=h_ps[:, j, :],
                         lhsT=wq[g][:, P * j : P * (j + 1)].bitcast(FP8X4),
                         lhsT_scale=wsc[g][:, P * j : P * (j + 1)],
-                        rhs=xg[g][:, tok].bitcast(FP8X4),
+                        rhs=x_codes[g].bitcast(FP8X4),
                         rhs_scale=xsg[4 * g : P, tok],
                         start=(g == 0),
                         stop=(g == PASSES - 1),
@@ -121,23 +127,27 @@ def tile_picked_ytop1_top1_p_kernel(tc, x_words, x_scales, w1, e_words, e_scales
             nc.vector.quantize_mx(out=hq[:].bitcast(FP8X4), scales=hs[:], in_=h_bf[:])
             return hq, hs
 
-        def scores(hq, hs):
-            banks = []
-            for h in range(U // BANK):
-                y_ps = psum.tile([P, BANK], F32, name="y_ps", bufs=4)
+        def scores(i, h):
+            hq, hs = quantised[i]
+            y_ps = psum.tile([P, BANK], F32, name="y_ps", tag="bank%d" % Y_BANKS[i][h])
+            col = 0
+            for words in eg[h]:
+                n = words.shape[1]
                 nc.tensor.matmul_mx(
-                    out=y_ps[:], lhsT=hq[:].bitcast(FP8X4), lhsT_scale=hs[:],
-                    rhs=eg[h][:].bitcast(FP8X4), rhs_scale=esg[h][:], start=True, stop=True,
+                    out=y_ps[:, col : col + n], lhsT=hq[:].bitcast(FP8X4), lhsT_scale=hs[:],
+                    rhs=words[:].bitcast(FP8X4), rhs_scale=esg[h][:, col : col + n], start=True, stop=True,
                 )
-                banks.append(y_ps)
-            return banks
+                col += n
+            return y_ps
 
         def sum_over_group(acc, terms):
             for d in range(D):
                 nc.tensor.matmul(acc, lhsT=terms[:, d, :], rhs=ident[:], is_transpose=True, start=(d == 0), stop=(d == D - 1))
 
-        def loss(i, banks):
-            last = i + 1 == TILES
+        halves = [slice(GROUPS * h, GROUPS * (h + 1)) for h in range(U // BANK)]
+        wide = [P, D, GROUPS]
+
+        def tiles_of():
             top = work.tile([P, V], F32, name="top")
             below = work.tile([P, D, V], F32, name="below")
             ex = work.tile([P, D, V], F32, name="ex")
@@ -145,85 +155,155 @@ def tile_picked_ytop1_top1_p_kernel(tc, x_words, x_scales, w1, e_words, e_scales
             th = work.tile([P, 2 * D, V], F32, name="th")
             both = work.tile([P, D, V], F32, name="both")
             z = work.tile([P, D, V], F32, name="z")
-            wide = [P, D, GROUPS]
-            halves = [slice(GROUPS * h, GROUPS * (h + 1)) for h in range(len(banks))]
+            return {"top": top, "below": below, "ex": ex, "args": args, "th": th, "both": both, "z": z}
 
-            def y_dv(h):
-                return banks[h][:].rearrange("p (v d) -> p d v", d=D)
+        def by_member(y_ps):
+            return y_ps[:].rearrange("p (v d) -> p d v", d=D)
 
-            def gate_args(h):
-                vs = halves[h]
-                nc.vector.tensor_tensor(args[:, :D, vs], y_dv(h), pos_sb[:, i, vs].unsqueeze(1).to_broadcast(wide), ALU.subtract)
-                nc.scalar.activation(args[:, D:, vs], y_dv(h), ACT.Square)
+        def minus_pos(i, t, y_ps, vs):
+            nc.vector.tensor_tensor(t["args"][:, :D, vs], by_member(y_ps), pos_sb[:, i, vs].unsqueeze(1).to_broadcast(wide), ALU.subtract)
 
-            def softmax_terms(h):
-                vs = halves[h]
-                nc.vector.tensor_reduce(top[:, vs], banks[h][:].rearrange("p (v d) -> p v d", d=D), mybir.AxisListType.X, ALU.max)
-                nc.vector.tensor_tensor(below[:, :, vs], y_dv(h), top[:, vs].unsqueeze(1).to_broadcast(wide), ALU.subtract)
-                nc.scalar.activation(ex[:, :, vs], below[:, :, vs], ACT.Exp)
+        def squares(t, y_ps, vs):
+            nc.scalar.activation(t["args"][:, D:, vs], by_member(y_ps), ACT.Square)
 
-            def gates(vs):
-                nc.scalar.activation(th[:, :, vs], args[:, :, vs], ACT.Tanh, scale=0.5)
+        def minus_top(t, y_ps, vs):
+            nc.vector.tensor_reduce(t["top"][:, vs], y_ps[:].rearrange("p (v d) -> p v d", d=D), mybir.AxisListType.X, ALU.max)
+            nc.vector.tensor_tensor(t["below"][:, :, vs], by_member(y_ps), t["top"][:, vs].unsqueeze(1).to_broadcast(wide), ALU.subtract)
 
-            def inverse_total():
-                total = psum.tile([P, P], F32, name="total", tag=H_BANKS[i % 2])
-                sum_over_group(total[:], ex)
-                inv = work.tile([P, P], F32, name="inv")
-                nc.vector.reciprocal(inv[:], total[:])
-                return inv
+        def exps(t, vs):
+            nc.scalar.activation(t["ex"][:, :, vs], t["below"][:, :, vs], ACT.Exp)
 
-            if not last:
-                for h, vs in enumerate(halves):
-                    gate_args(h)
-                    gates(vs)
-                    softmax_terms(h)
-                    nc.gpsimd.tensor_tensor(both[:, :, vs], th[:, :D, vs], th[:, D:, vs], ALU.add)
-                    nc.gpsimd.tensor_tensor(z[:, :, vs], both[:, :, vs], ex[:, :, vs], ALU.mult)
-                inv = inverse_total()
-                num = psum.tile([P, P], F32, name="num")
-                sum_over_group(num[:], z)
-                ratio = work.tile([P, P], F32, name="ratio")
-                nc.vector.tensor_tensor(ratio[:], num[:], inv[:], ALU.mult)
-                back = psum.tile([P, P], F32, name="back")
-                nc.tensor.transpose(back[:], ratio[:], ident[:])
-                res = work.tile([P, V], F32, name="res")
-                nc.scalar.activation(res[:], back[:], ACT.Copy, bias=1.0, scale=0.5)
-                nc.sync.dma_start(out[P * i : P * (i + 1), :], res[:])
-                return
+        def gates(t, vs):
+            nc.scalar.activation(t["th"][:, :, vs], t["args"][:, :, vs], ACT.Tanh, scale=0.5)
 
-            for h in range(len(banks)):
-                softmax_terms(h)
-            for h in range(len(banks)):
-                gate_args(h)
-            inv = inverse_total()
-            back = psum.tile([P, P], F32, name="back")
-            nc.tensor.transpose(back[:], inv[:], ident[:])
-            vs = halves[0]
-            gates(vs)
-            nc.gpsimd.tensor_tensor(both[:, :, vs], th[:, :D, vs], th[:, D:, vs], ALU.add)
-            nc.gpsimd.tensor_tensor(z[:, :, vs], both[:, :, vs], ex[:, :, vs], ALU.mult)
-            pieces = [slice(GROUPS + TAIL * c, GROUPS + TAIL * (c + 1)) for c in range(GROUPS // TAIL)]
-            for piece in pieces:
-                gates(piece)
-            num_sb = work.tile([P, V], F32, name="num_sb")
-            ratio = work.tile([P, GROUPS], F32, name="ratio_half")
-            res = work.tile([P, V], F32, name="res")
-            for piece in pieces:
-                nc.vector.tensor_tensor(both[:, :, piece], th[:, :D, piece], th[:, D:, piece], ALU.add)
-                nc.vector.scalar_tensor_tensor(z[:, :, piece], both[:, :, piece], 2.0, ex[:, :, piece], ALU.add, ALU.mult)
-                nc.vector.tensor_reduce(num_sb[:, piece], z[:, :, piece].rearrange("p d v -> p v d"), mybir.AxisListType.X, ALU.add)
-            nc.vector.scalar_tensor_tensor(res[:, halves[1]], num_sb[:, halves[1]], 0.5, back[:, halves[1]], ALU.mult, ALU.mult)
-            nc.vector.tensor_reduce(num_sb[:, vs], z[:, :, vs].rearrange("p d v -> p v d"), mybir.AxisListType.X, ALU.add)
-            nc.vector.tensor_tensor(ratio[:], num_sb[:, vs], back[:, vs], ALU.mult)
-            nc.scalar.activation(res[:, vs], ratio[:], ACT.Copy, bias=1.0, scale=0.5)
-            nc.sync.dma_start(out[P * i : P * (i + 1), :], res[:])
+        def add_gates(engine, t, vs):
+            engine.tensor_tensor(t["both"][:, :, vs], t["th"][:, :D, vs], t["th"][:, D:, vs], ALU.add)
+
+        def weigh(t, vs):
+            nc.gpsimd.tensor_tensor(t["z"][:, :, vs], t["both"][:, :, vs], t["ex"][:, :, vs], ALU.mult)
+
+        def split(vs):
+            return [slice(a, a + TAIL) for a in range(vs.start, vs.stop, TAIL)]
+
+        def inverses(totals):
+            first = work.tile([P, P], F32, name="first")
+            nc.vector.tensor_copy(first[:], totals[:, 0, :])
+            prod = work.tile([P, P], F32, name="prod")
+            nc.vector.tensor_tensor(prod[:], totals[:, 1, :], first[:], ALU.mult)
+            inv_prod = keep.tile([P, P], F32, name="inv_prod", tag="inv_prod")
+            nc.vector.reciprocal(inv_prod[:], prod[:])
+            inv = work.tile([P, 2, P], F32, name="inv")
+            nc.vector.tensor_tensor(inv[:], totals[:, :2, :], inv_prod[:].unsqueeze(1).to_broadcast([P, 2, P]), ALU.mult)
+            return inv
 
         quantised = [hidden(0)]
-        eg.append(keep.tile([P, BANK], U32, name="eg1", tag="h_bf0", align_bytes=64))
+        eg[1].append(keep.tile([P, BANK], U32, name="eg1", tag="h_bf0", align_bytes=64))
+        banks = {(0, 0): scores(0, 0)}
+        nc.vector.tensor_copy(eg[1][0][:], ew[:].indirect(neg_cols(1)))
+        ts = [tiles_of() for i in range(TILES)]
+        t0, t1, t2, t3 = ts
+        order = [(i, h) for i in range(TILES) for h in range(2)]
+
+        def gate_sum(i, h, pieces):
+            for piece in pieces:
+                gates(ts[i], piece)
+                add_gates(nc.gpsimd, ts[i], piece)
+
+        def square(k):
+            i, h = order[k]
+            squares(ts[i], banks[i, h], halves[h])
+
+        square(0)
+        minus_pos(0, t0, banks[0, 0], halves[0])
         quantised.extend(hidden(i) for i in range(1, TILES))
-        nc.vector.tensor_copy(eg[1][:], ew[:].indirect(neg_cols(1)))
-        banks = [scores(*quantised[0])]
-        for i in range(TILES):
-            if i + 1 < TILES:
-                banks.append(scores(*quantised[i + 1]))
-            loss(i, banks[i])
+        banks[0, 1] = scores(0, 1)
+        gate_sum(0, 0, split(halves[0]))
+        for i in range(1, TILES - 1):
+            for h in range(2):
+                banks[i, h] = scores(i, h)
+        square(1)
+        minus_top(t0, banks[0, 0], halves[0])
+        exps(t0, halves[0])
+        weigh(t0, halves[0])
+        for k in range(1, 5):
+            i, h = order[k]
+            t, vs = ts[i], halves[h]
+            minus_pos(i, t, banks[i, h], vs)
+            if k + 1 < SQUARE_FIRST:
+                square(k + 1)
+            minus_top(t, banks[i, h], vs)
+            if k >= SQUARE_FIRST:
+                square(k)
+            gate_sum(i, h, [vs])
+            exps(t, vs)
+            weigh(t, vs)
+            if i == 0:
+                for h in range(2):
+                    banks[3, h] = scores(3, h)
+                totals01 = psum.tile([P, 2, P], F32, name="totals", tag="bank0")
+                sum_over_group(totals01[:, 0, :], t0["ex"])
+            if (i, h) == (1, 1):
+                sum_over_group(totals01[:, 1, :], t1["ex"])
+        vs = halves[1]
+        minus_pos(2, t2, banks[2, 1], vs)
+        minus_top(t2, banks[2, 1], vs)
+        exps(t2, vs)
+        totals = psum.tile([P, 2, P], F32, name="totals", tag="bank1")
+        sum_over_group(totals[:, 0, :], t2["ex"])
+        if SQUARE_FIRST <= 5:
+            square(5)
+        for h, vs in enumerate(halves):
+            minus_top(t3, banks[3, h], vs)
+        for c in range(2):
+            turned = psum.tile([P, D // 2, P], F32, name="turned", tag="bank%d" % (6 + c))
+            for d in range(D // 2):
+                nc.tensor.transpose(turned[:, d, :], t3["below"][:, D // 2 * c + d, :], ident[:])
+            nc.scalar.activation(t3["ex"][:, D // 2 * c : D // 2 * (c + 1), :], turned[:], ACT.Exp)
+        sum_over_group(totals[:, 1, :], t3["ex"])
+        gate_sum(2, 1, [halves[1]])
+        weigh(t2, halves[1])
+        for h, vs in enumerate(halves):
+            minus_pos(3, t3, banks[3, h], vs)
+            squares(t3, banks[3, h], vs)
+        inv01 = inverses(totals01)
+
+        back = psum.tile([P, 2, P], F32, name="back", tag="bank0")
+        for a in range(2):
+            num = psum.tile([P, P], F32, name="num", tag="bank%d" % (4, 7)[a])
+            sum_over_group(num[:], ts[a]["z"])
+            ratio = work.tile([P, P], F32, name="ratio")
+            nc.vector.tensor_tensor(ratio[:], num[:], inv01[:, 1 - a, :], ALU.mult)
+            nc.tensor.transpose(back[:, a, :], ratio[:], ident[:])
+
+        inv = inverses(totals)
+        inv2 = psum.tile([P, P], F32, name="inv2", tag="bank1")
+        nc.tensor.transpose(inv2[:], inv[:, 1, :], ident[:])
+        n = D // LAST_PIECES
+        num3 = psum.tile([P, P], F32, name="num3", tag="bank6")
+        args3 = t3["args"][:].rearrange("p (k d) v -> p k d v", k=2)
+        th3 = t3["th"][:].rearrange("p (k d) v -> p k d v", k=2)
+        for c in range(LAST_PIECES):
+            ds = slice(n * c, n * (c + 1))
+            nc.scalar.activation(th3[:, :, ds, :], args3[:, :, ds, :], ACT.Tanh, scale=0.5)
+            gate_sums = psum.tile([P, n, P], F32, name="gate_sums", tag="bank%d" % (2, 3, 5, 4)[c])
+            for d in range(n):
+                for k in range(2):
+                    nc.tensor.matmul(gate_sums[:, d, :], lhsT=th3[:, k, n * c + d, :], rhs=ident[:], is_transpose=True, start=(k == 0), stop=(k == 1))
+            nc.vector.scalar_tensor_tensor(t3["z"][:, ds, :], gate_sums[:], 2.0, t3["ex"][:, ds, :], ALU.add, ALU.mult)
+            for d in range(n * c, n * (c + 1)):
+                nc.tensor.matmul(num3[:], lhsT=t3["z"][:, d, :], rhs=ident[:], is_transpose=True, start=(d == 0), stop=(d == D - 1))
+        res3 = work.tile([P, V], F32, name="res3")
+        nc.vector.scalar_tensor_tensor(res3[:], num3[:], 0.5, inv[:, 0, :], ALU.mult, ALU.mult)
+        nc.sync.dma_start(out[3 * P :, :], res3[:])
+
+        res = work.tile([P, 2, V], F32, name="res")
+        nc.scalar.activation(res[:], back[:], ACT.Copy, bias=1.0, scale=0.5)
+        nc.sync.dma_start(out[: 2 * P, :].rearrange("(a p) v -> p a v", p=P), res[:])
+
+        num2 = keep.tile([P, V], F32, name="num2", tag="inv_prod")
+        nc.vector.tensor_reduce(num2[:], t2["z"][:].rearrange("p d v -> p v d"), mybir.AxisListType.X, ALU.add)
+        ratio = work.tile([P, P], F32, name="ratio")
+        nc.vector.tensor_tensor(ratio[:], num2[:], inv2[:], ALU.mult)
+        res2 = work.tile([P, V], F32, name="res2")
+        nc.scalar.activation(res2[:], ratio[:], ACT.Copy, bias=1.0, scale=0.5)
+        nc.sync.dma_start(out[2 * P : 3 * P, :], res2[:])

@@ -147,11 +147,11 @@ def tile_picked_ytop1_top1_p_kernel(tc, x_words, x_scales, w1, e_words, e_scales
         halves = [slice(GROUPS * h, GROUPS * (h + 1)) for h in range(U // BANK)]
         wide = [P, D, GROUPS]
 
-        def tiles_of():
+        def tiles_of(i):
             top = work.tile([P, V], F32, name="top")
             below = work.tile([P, D, V], F32, name="below")
-            ex = work.tile([P, D, V], F32, name="ex")
-            args = work.tile([P, 2 * D, V], F32, name="args")
+            ex = keep.tile([P, D, V], F32, name="ex", tag="ex%d" % i)
+            args = keep.tile([P, 2 * D, V], F32, name="args", tag="args%d" % i)
             th = work.tile([P, 2 * D, V], F32, name="th")
             both = work.tile([P, D, V], F32, name="both")
             z = work.tile([P, D, V], F32, name="z")
@@ -185,14 +185,14 @@ def tile_picked_ytop1_top1_p_kernel(tc, x_words, x_scales, w1, e_words, e_scales
         def split(vs):
             return [slice(a, a + TAIL) for a in range(vs.start, vs.stop, TAIL)]
 
-        def inverses(totals):
-            first = work.tile([P, P], F32, name="first")
+        def inverses(totals, first_tag, inv_tag):
+            first = keep.tile([P, P], F32, name="first", tag=first_tag)
             nc.vector.tensor_copy(first[:], totals[:, 0, :])
             prod = work.tile([P, P], F32, name="prod")
             nc.vector.tensor_tensor(prod[:], totals[:, 1, :], first[:], ALU.mult)
-            inv_prod = keep.tile([P, P], F32, name="inv_prod", tag="inv_prod")
+            inv_prod = work.tile([P, P], F32, name="inv_prod")
             nc.vector.reciprocal(inv_prod[:], prod[:])
-            inv = work.tile([P, 2, P], F32, name="inv")
+            inv = keep.tile([P, 2, P], F32, name="inv", tag=inv_tag)
             nc.vector.tensor_tensor(inv[:], totals[:, :2, :], inv_prod[:].unsqueeze(1).to_broadcast([P, 2, P]), ALU.mult)
             return inv
 
@@ -200,7 +200,7 @@ def tile_picked_ytop1_top1_p_kernel(tc, x_words, x_scales, w1, e_words, e_scales
         eg[1].append(keep.tile([P, BANK], U32, name="eg1", tag="h_bf0", align_bytes=64))
         banks = {(0, 0): scores(0, 0)}
         nc.vector.tensor_copy(eg[1][0][:], ew[:].indirect(neg_cols(1)))
-        ts = [tiles_of() for i in range(TILES)]
+        ts = [tiles_of(i) for i in range(TILES)]
         t0, t1, t2, t3 = ts
         order = [(i, h) for i in range(TILES) for h in range(2)]
 
@@ -225,85 +225,105 @@ def tile_picked_ytop1_top1_p_kernel(tc, x_words, x_scales, w1, e_words, e_scales
         minus_top(t0, banks[0, 0], halves[0])
         exps(t0, halves[0])
         weigh(t0, halves[0])
-        for k in range(1, 5):
+        for k in range(1, 4):
             i, h = order[k]
             t, vs = ts[i], halves[h]
             minus_pos(i, t, banks[i, h], vs)
-            if k + 1 < SQUARE_FIRST:
-                square(k + 1)
+            square(k + 1)
             minus_top(t, banks[i, h], vs)
-            if k >= SQUARE_FIRST:
-                square(k)
             gate_sum(i, h, [vs])
             exps(t, vs)
             weigh(t, vs)
             if i == 0:
                 for h in range(2):
                     banks[3, h] = scores(3, h)
-                totals01 = psum.tile([P, 2, P], F32, name="totals", tag="bank0")
+                totals01 = psum.tile([P, 2, P], F32, name="totals01", tag="bank0")
                 sum_over_group(totals01[:, 0, :], t0["ex"])
-            if (i, h) == (1, 1):
-                sum_over_group(totals01[:, 1, :], t1["ex"])
-        vs = halves[1]
-        minus_pos(2, t2, banks[2, 1], vs)
-        minus_top(t2, banks[2, 1], vs)
-        exps(t2, vs)
-        totals = psum.tile([P, 2, P], F32, name="totals", tag="bank1")
-        sum_over_group(totals[:, 0, :], t2["ex"])
-        if SQUARE_FIRST <= 5:
-            square(5)
+
         for h, vs in enumerate(halves):
             minus_top(t3, banks[3, h], vs)
+        minus_pos(2, t2, banks[2, 0], halves[0])
+        sum_over_group(totals01[:, 1, :], t1["ex"])
+        gate_sum(2, 0, [halves[0]])
+        square(5)
+        square(6)
+        square(7)
         for c in range(2):
-            turned = psum.tile([P, D // 2, P], F32, name="turned", tag="bank%d" % (6 + c))
+            turned = psum.tile([P, D // 2, P], F32, name="turned", tag="bank%d" % (4 + c))
             for d in range(D // 2):
                 nc.tensor.transpose(turned[:, d, :], t3["below"][:, D // 2 * c + d, :], ident[:])
             nc.scalar.activation(t3["ex"][:, D // 2 * c : D // 2 * (c + 1), :], turned[:], ACT.Exp)
-        sum_over_group(totals[:, 1, :], t3["ex"])
+
+        minus_top(t2, banks[2, 0], halves[0])
+        minus_pos(2, t2, banks[2, 1], halves[1])
+        exps(t2, halves[0])
+        weigh(t2, halves[0])
+        inv01 = inverses(totals01, "first01", "inv01")
+        minus_top(t2, banks[2, 1], halves[1])
+
+        exps(t2, halves[1])
         gate_sum(2, 1, [halves[1]])
         weigh(t2, halves[1])
-        for h, vs in enumerate(halves):
-            minus_pos(3, t3, banks[3, h], vs)
-            squares(t3, banks[3, h], vs)
-        inv01 = inverses(totals01)
+        totals32 = psum.tile([P, 2, P], F32, name="totals32", tag="bank6")
+        sum_over_group(totals32[:, 0, :], t3["ex"])
+        sum_over_group(totals32[:, 1, :], t2["ex"])
+        for k in range(6, 8):
 
-        back = psum.tile([P, 2, P], F32, name="back", tag="bank0")
+            i, h = order[k]
+            minus_pos(i, ts[i], banks[i, h], halves[h])
+
+        nums = []
         for a in range(2):
-            num = psum.tile([P, P], F32, name="num", tag="bank%d" % (4, 7)[a])
+            num = psum.tile([P, P], F32, name="num", tag="bank%d" % (1, 7)[a])
             sum_over_group(num[:], ts[a]["z"])
             ratio = work.tile([P, P], F32, name="ratio")
             nc.vector.tensor_tensor(ratio[:], num[:], inv01[:, 1 - a, :], ALU.mult)
-            nc.tensor.transpose(back[:, a, :], ratio[:], ident[:])
+            nums.append(ratio)
+        back = psum.tile([P, 2, P], F32, name="back", tag="bank1")
+        for a in range(2):
+            nc.tensor.transpose(back[:, a, :], nums[a][:], ident[:])
+        inv = inverses(totals32, "inv01", "inv32")
+        inv2 = psum.tile([P, P], F32, name="inv2", tag="bank7")
+        nc.tensor.transpose(inv2[:], inv[:, 0, :], ident[:])
 
-        inv = inverses(totals)
-        inv2 = psum.tile([P, P], F32, name="inv2", tag="bank1")
-        nc.tensor.transpose(inv2[:], inv[:, 1, :], ident[:])
         n = D // LAST_PIECES
-        num3 = psum.tile([P, P], F32, name="num3", tag="bank6")
+        num3 = psum.tile([P, P], F32, name="num3", tag="bank0")
         args3 = t3["args"][:].rearrange("p (k d) v -> p k d v", k=2)
         th3 = t3["th"][:].rearrange("p (k d) v -> p k d v", k=2)
+        part = work.tile([P, D // 2, V], F32, name="part")
+
+        def fold(step):
+            if step == 0:
+                nc.gpsimd.tensor_tensor(part[:], t2["z"][:, : D // 2, :], t2["z"][:, D // 2 :, :], ALU.add)
+            else:
+                m = D // 2 >> step
+                nc.gpsimd.tensor_tensor(part[:, :m, :], part[:, :m, :], part[:, m : 2 * m, :], ALU.add)
+
+        sums = []
         for c in range(LAST_PIECES):
             ds = slice(n * c, n * (c + 1))
             nc.scalar.activation(th3[:, :, ds, :], args3[:, :, ds, :], ACT.Tanh, scale=0.5)
-            gate_sums = psum.tile([P, n, P], F32, name="gate_sums", tag="bank%d" % (2, 3, 5, 4)[c])
+            gate_sums = psum.tile([P, n, P], F32, name="gate_sums", tag="bank%d" % (4, 5, 2, 3)[c])
             for d in range(n):
                 for k in range(2):
                     nc.tensor.matmul(gate_sums[:, d, :], lhsT=th3[:, k, n * c + d, :], rhs=ident[:], is_transpose=True, start=(k == 0), stop=(k == 1))
-            nc.vector.scalar_tensor_tensor(t3["z"][:, ds, :], gate_sums[:], 2.0, t3["ex"][:, ds, :], ALU.add, ALU.mult)
-            for d in range(n * c, n * (c + 1)):
-                nc.tensor.matmul(num3[:], lhsT=t3["z"][:, d, :], rhs=ident[:], is_transpose=True, start=(d == 0), stop=(d == D - 1))
-        res3 = work.tile([P, V], F32, name="res3")
-        nc.vector.scalar_tensor_tensor(res3[:], num3[:], 0.5, inv[:, 0, :], ALU.mult, ALU.mult)
-        nc.sync.dma_start(out[3 * P :, :], res3[:])
-
+            sums.append(gate_sums)
         res = work.tile([P, 2, V], F32, name="res")
         nc.scalar.activation(res[:], back[:], ACT.Copy, bias=1.0, scale=0.5)
         nc.sync.dma_start(out[: 2 * P, :].rearrange("(a p) v -> p a v", p=P), res[:])
+        for step in range(3):
+            fold(step)
+        for c in range(LAST_PIECES):
+            ds = slice(n * c, n * (c + 1))
+            nc.vector.scalar_tensor_tensor(t3["z"][:, ds, :], sums[c][:], 2.0, t3["ex"][:, ds, :], ALU.add, ALU.mult)
+            for d in range(n * c, n * (c + 1)):
+                nc.tensor.matmul(num3[:], lhsT=t3["z"][:, d, :], rhs=ident[:], is_transpose=True, start=(d == 0), stop=(d == D - 1))
 
-        num2 = keep.tile([P, V], F32, name="num2", tag="inv_prod")
-        nc.vector.tensor_reduce(num2[:], t2["z"][:].rearrange("p d v -> p v d"), mybir.AxisListType.X, ALU.add)
-        ratio = work.tile([P, P], F32, name="ratio")
-        nc.vector.tensor_tensor(ratio[:], num2[:], inv2[:], ALU.mult)
+        ratio2 = keep.tile([P, V], F32, name="ratio2", tag="ex3")
+        nc.vector.tensor_tensor(ratio2[:], inv2[:], part[:, 0, :], ALU.mult)
         res2 = work.tile([P, V], F32, name="res2")
-        nc.scalar.activation(res2[:], ratio[:], ACT.Copy, bias=1.0, scale=0.5)
+        nc.scalar.activation(res2[:], ratio2[:], ACT.Copy, bias=1.0, scale=0.5)
         nc.sync.dma_start(out[2 * P : 3 * P, :], res2[:])
+        res3 = work.tile([P, V], F32, name="res3")
+        nc.vector.scalar_tensor_tensor(res3[:], num3[:], 0.5, inv[:, 1, :], ALU.mult, ALU.mult)
+        nc.sync.dma_start(out[3 * P :, :], res3[:])

@@ -22,7 +22,7 @@ PASSES = K // (P * PACK)
 BANK = 512
 GROUPS = BANK // D
 TILES = S // P
-M_SPLIT = 80
+M_SPLIT = 72
 SQUARE_FIRST = 5
 LAST_PIECES = 4
 TAIL = 32
@@ -99,6 +99,12 @@ def tile_picked_ytop1_top1_p_kernel(tc, x_words, x_scales, w1, e_words, e_scales
         nc.vector.tensor_copy(xg0[:], xw[0][:].indirect(offs_sb[:]))
         nc.vector.tensor_copy(xsg[:], xs[:].indirect(offs_sb[:]))
         quantize_w1(0, P, 1)
+        warm = psum.tile([P, BANK], F32, name="warm", tag="bank7")
+        for n in (512, 256):
+            nc.tensor.matmul_mx(
+                out=warm[:, :n], lhsT=wq[0][:, :P].bitcast(FP8X4), lhsT_scale=wsc[0][:, :P],
+                rhs=xg0[:, :n].bitcast(FP8X4), rhs_scale=xsg[:, :n], start=True, stop=True,
+            )
         nc.vector.tensor_copy(xg1_first[:], xw[1][:].indirect(offs_sb[:, : P // 16]))
         quantize_w1(1, M_SPLIT, 4)
         xg1_rest = keep.tile([P, S - P], U32, name="xg1_rest", tag="w_raw1", align_bytes=64)
@@ -264,9 +270,10 @@ def tile_picked_ytop1_top1_p_kernel(tc, x_words, x_scales, w1, e_words, e_scales
         exps(t2, halves[1])
         gate_sum(2, 1, [halves[1]])
         weigh(t2, halves[1])
-        totals32 = psum.tile([P, 2, P], F32, name="totals32", tag="bank6")
-        sum_over_group(totals32[:, 0, :], t3["ex"])
-        sum_over_group(totals32[:, 1, :], t2["ex"])
+        total3 = psum.tile([P, P], F32, name="total3", tag="bank6")
+        sum_over_group(total3[:], t3["ex"])
+        total2 = psum.tile([P, P], F32, name="total2", tag="bank0")
+        sum_over_group(total2[:], t2["ex"])
         for k in range(6, 8):
 
             i, h = order[k]
@@ -282,12 +289,15 @@ def tile_picked_ytop1_top1_p_kernel(tc, x_words, x_scales, w1, e_words, e_scales
         back = psum.tile([P, 2, P], F32, name="back", tag="bank1")
         for a in range(2):
             nc.tensor.transpose(back[:, a, :], nums[a][:], ident[:])
-        inv = inverses(totals32, "inv01", "inv32")
+        inv3 = work.tile([P, P], F32, name="inv3")
+        nc.vector.reciprocal(inv3[:], total3[:])
+        inv2_sb = work.tile([P, P], F32, name="inv2_sb")
+        nc.vector.reciprocal(inv2_sb[:], total2[:])
         inv2 = psum.tile([P, P], F32, name="inv2", tag="bank7")
-        nc.tensor.transpose(inv2[:], inv[:, 0, :], ident[:])
+        nc.tensor.transpose(inv2[:], inv2_sb[:], ident[:])
 
         n = D // LAST_PIECES
-        num3 = psum.tile([P, P], F32, name="num3", tag="bank0")
+        num3 = psum.tile([P, P], F32, name="num3", tag="bank6")
         args3 = t3["args"][:].rearrange("p (k d) v -> p k d v", k=2)
         th3 = t3["th"][:].rearrange("p (k d) v -> p k d v", k=2)
         part = work.tile([P, D // 2, V], F32, name="part")
@@ -311,7 +321,7 @@ def tile_picked_ytop1_top1_p_kernel(tc, x_words, x_scales, w1, e_words, e_scales
         res = work.tile([P, 2, V], F32, name="res")
         nc.scalar.activation(res[:], back[:], ACT.Copy, bias=1.0, scale=0.5)
         nc.sync.dma_start(out[: 2 * P, :].rearrange("(a p) v -> p a v", p=P), res[:])
-        for step in range(3):
+        for step in range(1):
             fold(step)
         for c in range(LAST_PIECES):
             ds = slice(n * c, n * (c + 1))
@@ -319,11 +329,15 @@ def tile_picked_ytop1_top1_p_kernel(tc, x_words, x_scales, w1, e_words, e_scales
             for d in range(n * c, n * (c + 1)):
                 nc.tensor.matmul(num3[:], lhsT=t3["z"][:, d, :], rhs=ident[:], is_transpose=True, start=(d == 0), stop=(d == D - 1))
 
-        ratio2 = keep.tile([P, V], F32, name="ratio2", tag="ex3")
-        nc.vector.tensor_tensor(ratio2[:], inv2[:], part[:, 0, :], ALU.mult)
+        half = keep.tile([P, 2, V], F32, name="half", tag="ex3")
+        nc.vector.tensor_tensor(half[:], part[:, :2, :], part[:, 2:, :], ALU.add)
+        num2 = work.tile([P, V], F32, name="num2")
+        nc.vector.tensor_tensor(num2[:], half[:, 0, :], half[:, 1, :], ALU.add)
+        ratio2 = work.tile([P, V], F32, name="ratio2")
+        nc.vector.tensor_tensor(ratio2[:], inv2[:], num2[:], ALU.mult)
         res2 = work.tile([P, V], F32, name="res2")
-        nc.scalar.activation(res2[:], ratio2[:], ACT.Copy, bias=1.0, scale=0.5)
+        nc.vector.tensor_scalar(res2[:], ratio2[:], 0.5, 1.0, ALU.mult, ALU.add)
         nc.sync.dma_start(out[2 * P : 3 * P, :], res2[:])
         res3 = work.tile([P, V], F32, name="res3")
-        nc.vector.scalar_tensor_tensor(res3[:], num3[:], 0.5, inv[:, 1, :], ALU.mult, ALU.mult)
+        nc.vector.scalar_tensor_tensor(res3[:], num3[:], 0.5, inv3[:], ALU.mult, ALU.mult)
         nc.sync.dma_start(out[3 * P :, :], res3[:])

@@ -22,10 +22,10 @@ PASSES = K // (P * PACK)
 BANK = 512
 GROUPS = BANK // D
 TILES = S // P
-M_SPLIT = 72
-SQUARE_FIRST = 5
+SCALAR_SHARE = (96, 64, 16)
 LAST_PIECES = 4
 TAIL = 32
+REACH = 30.0
 H_BANKS = (0, 1, 3, 1)
 Y_BANKS = ((2, 3), (4, 5), (6, 7), (2, 3))
 
@@ -43,7 +43,8 @@ def tile_picked_ytop1_top1_p_kernel(tc, x_words, x_scales, w1, e_words, e_scales
         xs = keep.tile([P, T], U8, name="xs", align_bytes=64)
         ew = keep.tile([P, W], U32, name="ew", align_bytes=64)
         es = keep.tile([P, W], U8, name="es", align_bytes=64)
-        w_raw = [keep.tile([P, PACK * H], F32, name="w_raw", tag="w_raw%d" % g, align_bytes=64) for g in range(PASSES)]
+        w_pieces = ((0, 0, H), (1, 0, H // 2), (1, H // 2, H // 2))
+        w_raw = [keep.tile([P, PACK, n], F32, name="w_raw%d" % c, align_bytes=64) for c, (g, first, n) in enumerate(w_pieces)]
         pos_sb = keep.tile([P, TILES, V], F32, name="pos_sb")
         ident = keep.tile([P, P], F32, name="ident")
 
@@ -53,18 +54,20 @@ def tile_picked_ytop1_top1_p_kernel(tc, x_words, x_scales, w1, e_words, e_scales
         def load_words(dst, words):
             nc.sync.dma_start(dst[:].bitcast(I32), words.rearrange("p n t -> p (n t)").bitcast(I32))
 
-        def load_w1(g):
-            nc.sync.dma_start(w_raw[g][:], w1[512 * g : 512 * (g + 1), :].rearrange("(p j) c -> p (j c)", j=PACK))
+        def load_w1(c):
+            g, first, n = w_pieces[c]
+            nc.sync.dma_start(w_raw[c][:], w1[512 * g : 512 * (g + 1), first : first + n].rearrange("(p j) c -> p j c", j=PACK))
 
         nc.sync.dma_start(offs_sb[:], offs)
         nc.sync.dma_start(neg_sb[:], neg)
         for q in range(4):
             nc.sync.dma_start(es[32 * q : 32 * q + 4, :].bitcast(I32), e_scales[0, 4 * q : 4 * q + 4, :].bitcast(I32))
         load_w1(0)
-        load_words(xw[0], x_words[0])
         for q in range(4):
             nc.sync.dma_start(xs[32 * q : 32 * q + 4 * PASSES, :].bitcast(I32), x_scales[:, 4 * q : 4 * q + 4, :].bitcast(I32))
+        load_words(xw[0], x_words[0])
         load_w1(1)
+        load_w1(2)
         load_words(xw[1], x_words[1])
         load_words(ew, e_words[0])
         nc.sync.dma_start(pos_sb[:], pos.rearrange("(a p) v -> p a v", p=P))
@@ -76,38 +79,41 @@ def tile_picked_ytop1_top1_p_kernel(tc, x_words, x_scales, w1, e_words, e_scales
         xsg = keep.tile([P, S], U8, name="xsg", align_bytes=64)
         eg = [[keep.tile([P, BANK], U32, name="eg0", align_bytes=64)], []]
         esg = [keep.tile([P, BANK], U8, name="esg%d" % h, align_bytes=64) for h in range(U // BANK)]
-        wq = [keep.tile([P, H], U32, name="wq%d" % g, align_bytes=64) for g in range(PASSES)]
+        wq = {}
         wsc = [keep.tile([P, H], U8, name="wsc%d" % g, align_bytes=64) for g in range(PASSES)]
 
         def neg_cols(h):
             return neg_sb[:, h * BANK // 16 : (h + 1) * BANK // 16]
 
-        def quantize_w1(g, m_split, pieces):
-            w_bf = keep.tile([P, PACK * H], BF16, name="w_bf", tag="w_bf%d" % g, align_bytes=64)
-            dst = w_bf[:].rearrange("p (t m j) -> p m t j", t=PACK, j=PACK)
-            src = w_raw[g][:].rearrange("p (j m t) -> p m t j", j=PACK, t=PACK)
+        w_bf = [keep.tile([P, PACK * H], BF16, name="w_bf%d" % g, align_bytes=64) for g in range(PASSES)]
+
+        def cast_w1(c):
+            g, first, n = w_pieces[c]
+            dst = w_bf[g][:].rearrange("p (t m j) -> p m t j", t=PACK, j=PACK)[:, first // PACK : (first + n) // PACK]
+            src = w_raw[c][:].rearrange("p j (m t) -> p m t j", t=PACK)
+            m_split = SCALAR_SHARE[c]
             nc.scalar.activation(dst[:, :m_split], src[:, :m_split], ACT.Copy)
-            if m_split < P:
+            if m_split < n // PACK:
                 nc.vector.tensor_copy(dst[:, m_split:], src[:, m_split:])
+
+        def quantize_w1(g, pieces):
             n = H // pieces
+            wq[g] = keep.tile([P, H], U32, name="wq%d" % g, tag="xw0" if g == 0 else "wq1", align_bytes=64)
             for c in range(pieces):
                 cols = slice(n * c, n * (c + 1))
-                nc.vector.quantize_mx(out=wq[g][:, cols].bitcast(FP8X4), scales=wsc[g][:, cols], in_=w_bf[:, PACK * n * c : PACK * n * (c + 1)])
+                nc.vector.quantize_mx(out=wq[g][:, cols].bitcast(FP8X4), scales=wsc[g][:, cols], in_=w_bf[g][:, PACK * n * c : PACK * n * (c + 1)])
 
         for h in range(U // BANK):
             nc.vector.tensor_copy(esg[h][:], es[:].indirect(neg_cols(h)))
-        nc.vector.tensor_copy(xg0[:], xw[0][:].indirect(offs_sb[:]))
+        cast_w1(0)
         nc.vector.tensor_copy(xsg[:], xs[:].indirect(offs_sb[:]))
-        quantize_w1(0, P, 1)
-        warm = psum.tile([P, BANK], F32, name="warm", tag="bank7")
-        for n in (512, 256):
-            nc.tensor.matmul_mx(
-                out=warm[:, :n], lhsT=wq[0][:, :P].bitcast(FP8X4), lhsT_scale=wsc[0][:, :P],
-                rhs=xg0[:, :n].bitcast(FP8X4), rhs_scale=xsg[:, :n], start=True, stop=True,
-            )
+        nc.vector.tensor_copy(xg0[:], xw[0][:].indirect(offs_sb[:]))
+        quantize_w1(0, 1)
+        cast_w1(1)
+        cast_w1(2)
+        quantize_w1(1, 2)
         nc.vector.tensor_copy(xg1_first[:], xw[1][:].indirect(offs_sb[:, : P // 16]))
-        quantize_w1(1, M_SPLIT, 4)
-        xg1_rest = keep.tile([P, S - P], U32, name="xg1_rest", tag="w_raw1", align_bytes=64)
+        xg1_rest = keep.tile([P, S - P], U32, name="xg1_rest", align_bytes=64)
         nc.vector.tensor_copy(xg1_rest[:], xw[1][:].indirect(offs_sb[:, P // 16 :]))
         nc.vector.tensor_copy(eg[0][0][:], ew[:].indirect(neg_cols(0)))
 
@@ -185,19 +191,20 @@ def tile_picked_ytop1_top1_p_kernel(tc, x_words, x_scales, w1, e_words, e_scales
         def add_gates(engine, t, vs):
             engine.tensor_tensor(t["both"][:, :, vs], t["th"][:, :D, vs], t["th"][:, D:, vs], ALU.add)
 
-        def weigh(t, vs):
-            nc.gpsimd.tensor_tensor(t["z"][:, :, vs], t["both"][:, :, vs], t["ex"][:, :, vs], ALU.mult)
+        def weigh(t, vs, engine=nc.gpsimd):
+            engine.tensor_tensor(t["z"][:, :, vs], t["both"][:, :, vs], t["ex"][:, :, vs], ALU.mult)
 
         def split(vs):
             return [slice(a, a + TAIL) for a in range(vs.start, vs.stop, TAIL)]
 
-        def inverses(totals, first_tag, inv_tag):
+        def inverses(totals, first_tag, inv_tag, kept, later_totals):
             first = keep.tile([P, P], F32, name="first", tag=first_tag)
             nc.vector.tensor_copy(first[:], totals[:, 0, :])
             prod = work.tile([P, P], F32, name="prod")
             nc.vector.tensor_tensor(prod[:], totals[:, 1, :], first[:], ALU.mult)
             inv_prod = work.tile([P, P], F32, name="inv_prod")
             nc.vector.reciprocal(inv_prod[:], prod[:])
+            nc.vector.tensor_copy(kept[:], later_totals[:, 0, :])
             inv = keep.tile([P, 2, P], F32, name="inv", tag=inv_tag)
             nc.vector.tensor_tensor(inv[:], totals[:, :2, :], inv_prod[:].unsqueeze(1).to_broadcast([P, 2, P]), ALU.mult)
             return inv
@@ -224,6 +231,12 @@ def tile_picked_ytop1_top1_p_kernel(tc, x_words, x_scales, w1, e_words, e_scales
         quantised.extend(hidden(i) for i in range(1, TILES))
         banks[0, 1] = scores(0, 1)
         gate_sum(0, 0, split(halves[0]))
+        pos_turned = psum.tile([P, P], F32, name="pos_turned", tag="bank0")
+        nc.tensor.transpose(pos_turned[:], pos_sb[:, 3, :], ident[:])
+        pos_turned_sb = keep.tile([P, P], F32, name="pos_turned_sb")
+        nc.scalar.activation(pos_turned_sb[:], pos_turned[:], ACT.Copy, bias=REACH)
+        raised = psum.tile([P, P], F32, name="raised", tag="bank1")
+        nc.tensor.transpose(raised[:], pos_turned_sb[:], ident[:])
         for i in range(1, TILES - 1):
             for h in range(2):
                 banks[i, h] = scores(i, h)
@@ -246,8 +259,14 @@ def tile_picked_ytop1_top1_p_kernel(tc, x_words, x_scales, w1, e_words, e_scales
                 totals01 = psum.tile([P, 2, P], F32, name="totals01", tag="bank0")
                 sum_over_group(totals01[:, 0, :], t0["ex"])
 
+        bounds = keep.tile([P, 2, V], F32, name="bounds")
+        shift = keep.tile([P, V], F32, name="shift")
         for h, vs in enumerate(halves):
-            minus_top(t3, banks[3, h], vs)
+            nc.vector.tensor_reduce(bounds[:, 0, vs], banks[3, h][:].rearrange("p (v d) -> p v d", d=D), mybir.AxisListType.X, ALU.max)
+        nc.vector.scalar_tensor_tensor(bounds[:, 1, :], bounds[:, 0, :], 2 * REACH, raised[:], ALU.add, ALU.min)
+        nc.vector.tensor_reduce(shift[:], bounds[:].rearrange("p r v -> p v r"), mybir.AxisListType.X, ALU.max)
+        for h, vs in enumerate(halves):
+            nc.vector.scalar_tensor_tensor(t3["args"][:, :D, vs], by_member(banks[3, h]), REACH, shift[:, vs].unsqueeze(1).to_broadcast(wide), ALU.add, ALU.subtract)
         minus_pos(2, t2, banks[2, 0], halves[0])
         sum_over_group(totals01[:, 1, :], t1["ex"])
         gate_sum(2, 0, [halves[0]])
@@ -257,27 +276,23 @@ def tile_picked_ytop1_top1_p_kernel(tc, x_words, x_scales, w1, e_words, e_scales
         for c in range(2):
             turned = psum.tile([P, D // 2, P], F32, name="turned", tag="bank%d" % (4 + c))
             for d in range(D // 2):
-                nc.tensor.transpose(turned[:, d, :], t3["below"][:, D // 2 * c + d, :], ident[:])
+                nc.tensor.transpose(turned[:, d, :], t3["args"][:, D // 2 * c + d, :], ident[:])
             nc.scalar.activation(t3["ex"][:, D // 2 * c : D // 2 * (c + 1), :], turned[:], ACT.Exp)
 
-        minus_top(t2, banks[2, 0], halves[0])
         minus_pos(2, t2, banks[2, 1], halves[1])
-        exps(t2, halves[0])
-        weigh(t2, halves[0])
-        inv01 = inverses(totals01, "first01", "inv01")
-        minus_top(t2, banks[2, 1], halves[1])
-
-        exps(t2, halves[1])
-        gate_sum(2, 1, [halves[1]])
-        weigh(t2, halves[1])
-        total3 = psum.tile([P, P], F32, name="total3", tag="bank6")
-        sum_over_group(total3[:], t3["ex"])
-        total2 = psum.tile([P, P], F32, name="total2", tag="bank0")
-        sum_over_group(total2[:], t2["ex"])
-        for k in range(6, 8):
-
-            i, h = order[k]
-            minus_pos(i, ts[i], banks[i, h], halves[h])
+        gates(t2, halves[1])
+        for h, vs in enumerate(halves):
+            minus_top(t2, banks[2, h], vs)
+        totals23 = psum.tile([P, 2, P], F32, name="totals23", tag="bank6")
+        sum_over_group(totals23[:, 0, :], t3["ex"])
+        first23 = keep.tile([P, P], F32, name="first23")
+        inv01 = inverses(totals01, "first01", "inv01", first23, totals23)
+        add_gates(nc.vector, t2, halves[1])
+        for c in range(2):
+            ds = slice(D // 2 * c, D // 2 * (c + 1))
+            nc.scalar.activation(t2["ex"][:, ds, :], t2["below"][:, ds, :], ACT.Exp)
+        nc.vector.tensor_tensor(t2["z"][:], t2["both"][:], t2["ex"][:], ALU.mult)
+        sum_over_group(totals23[:, 1, :], t2["ex"])
 
         nums = []
         for a in range(2):
@@ -289,15 +304,15 @@ def tile_picked_ytop1_top1_p_kernel(tc, x_words, x_scales, w1, e_words, e_scales
         back = psum.tile([P, 2, P], F32, name="back", tag="bank1")
         for a in range(2):
             nc.tensor.transpose(back[:, a, :], nums[a][:], ident[:])
-        inv3 = work.tile([P, P], F32, name="inv3")
-        nc.vector.reciprocal(inv3[:], total3[:])
-        inv2_sb = work.tile([P, P], F32, name="inv2_sb")
-        nc.vector.reciprocal(inv2_sb[:], total2[:])
-        inv2 = psum.tile([P, P], F32, name="inv2", tag="bank7")
-        nc.tensor.transpose(inv2[:], inv2_sb[:], ident[:])
+        prod23 = keep.tile([P, P], F32, name="prod23")
+        nc.vector.tensor_tensor(prod23[:], totals23[:, 1, :], first23[:], ALU.mult)
+        inv_prod23 = keep.tile([P, P], F32, name="inv_prod23")
+        nc.vector.reciprocal(inv_prod23[:], prod23[:])
+        inv23 = keep.tile([P, 2, P], F32, name="inv23")
+        nc.vector.tensor_tensor(inv23[:], totals23[:], inv_prod23[:].unsqueeze(1).to_broadcast([P, 2, P]), ALU.mult)
 
         n = D // LAST_PIECES
-        num3 = psum.tile([P, P], F32, name="num3", tag="bank6")
+        num3 = psum.tile([P, P], F32, name="num3", tag="bank0")
         args3 = t3["args"][:].rearrange("p (k d) v -> p k d v", k=2)
         th3 = t3["th"][:].rearrange("p (k d) v -> p k d v", k=2)
         part = work.tile([P, D // 2, V], F32, name="part")
@@ -329,15 +344,17 @@ def tile_picked_ytop1_top1_p_kernel(tc, x_words, x_scales, w1, e_words, e_scales
             for d in range(n * c, n * (c + 1)):
                 nc.tensor.matmul(num3[:], lhsT=t3["z"][:, d, :], rhs=ident[:], is_transpose=True, start=(d == 0), stop=(d == D - 1))
 
-        half = keep.tile([P, 2, V], F32, name="half", tag="ex3")
-        nc.vector.tensor_tensor(half[:], part[:, :2, :], part[:, 2:, :], ALU.add)
+        inv2 = psum.tile([P, P], F32, name="inv2", tag="bank4")
+        nc.tensor.transpose(inv2[:], inv23[:, 0, :], ident[:])
+        half = keep.tile([P, 2, V], F32, name="half")
+        nc.gpsimd.tensor_tensor(half[:], part[:, :2, :], part[:, 2:, :], ALU.add)
         num2 = work.tile([P, V], F32, name="num2")
-        nc.vector.tensor_tensor(num2[:], half[:, 0, :], half[:, 1, :], ALU.add)
+        nc.gpsimd.tensor_tensor(num2[:], half[:, 0, :], half[:, 1, :], ALU.add)
         ratio2 = work.tile([P, V], F32, name="ratio2")
         nc.vector.tensor_tensor(ratio2[:], inv2[:], num2[:], ALU.mult)
         res2 = work.tile([P, V], F32, name="res2")
         nc.vector.tensor_scalar(res2[:], ratio2[:], 0.5, 1.0, ALU.mult, ALU.add)
         nc.sync.dma_start(out[2 * P : 3 * P, :], res2[:])
         res3 = work.tile([P, V], F32, name="res3")
-        nc.vector.scalar_tensor_tensor(res3[:], num3[:], 0.5, inv3[:], ALU.mult, ALU.mult)
+        nc.vector.scalar_tensor_tensor(res3[:], num3[:], 0.5, inv23[:, 1, :], ALU.mult, ALU.mult)
         nc.sync.dma_start(out[3 * P :, :], res3[:])

@@ -231,12 +231,6 @@ def tile_picked_ytop1_top1_p_kernel(tc, x_words, x_scales, w1, e_words, e_scales
         quantised.extend(hidden(i) for i in range(1, TILES))
         banks[0, 1] = scores(0, 1)
         gate_sum(0, 0, split(halves[0]))
-        pos_turned = psum.tile([P, P], F32, name="pos_turned", tag="bank0")
-        nc.tensor.transpose(pos_turned[:], pos_sb[:, 3, :], ident[:])
-        pos_turned_sb = keep.tile([P, P], F32, name="pos_turned_sb")
-        nc.scalar.activation(pos_turned_sb[:], pos_turned[:], ACT.Copy, bias=REACH)
-        raised = psum.tile([P, P], F32, name="raised", tag="bank1")
-        nc.tensor.transpose(raised[:], pos_turned_sb[:], ident[:])
         for i in range(1, TILES - 1):
             for h in range(2):
                 banks[i, h] = scores(i, h)
@@ -244,6 +238,12 @@ def tile_picked_ytop1_top1_p_kernel(tc, x_words, x_scales, w1, e_words, e_scales
         minus_top(t0, banks[0, 0], halves[0])
         exps(t0, halves[0])
         weigh(t0, halves[0])
+        pos_turned = psum.tile([P, P], F32, name="pos_turned", tag="bank1")
+        nc.tensor.transpose(pos_turned[:], pos_sb[:, 3, :], ident[:])
+        pos_turned_sb = keep.tile([P, P], F32, name="pos_turned_sb")
+        nc.scalar.activation(pos_turned_sb[:], pos_turned[:], ACT.Copy, bias=REACH)
+        raised = psum.tile([P, P], F32, name="raised", tag="bank1")
+        nc.tensor.transpose(raised[:], pos_turned_sb[:], ident[:])
         for k in range(1, 4):
             i, h = order[k]
             t, vs = ts[i], halves[h]
@@ -291,7 +291,7 @@ def tile_picked_ytop1_top1_p_kernel(tc, x_words, x_scales, w1, e_words, e_scales
         for c in range(2):
             ds = slice(D // 2 * c, D // 2 * (c + 1))
             nc.scalar.activation(t2["ex"][:, ds, :], t2["below"][:, ds, :], ACT.Exp)
-        nc.vector.tensor_tensor(t2["z"][:], t2["both"][:], t2["ex"][:], ALU.mult)
+        nc.vector.scalar_tensor_tensor(t2["z"][:], t2["both"][:], 2.0, t2["ex"][:], ALU.add, ALU.mult)
         sum_over_group(totals23[:, 1, :], t2["ex"])
 
         nums = []
@@ -350,10 +350,8 @@ def tile_picked_ytop1_top1_p_kernel(tc, x_words, x_scales, w1, e_words, e_scales
         nc.gpsimd.tensor_tensor(half[:], part[:, :2, :], part[:, 2:, :], ALU.add)
         num2 = work.tile([P, V], F32, name="num2")
         nc.gpsimd.tensor_tensor(num2[:], half[:, 0, :], half[:, 1, :], ALU.add)
-        ratio2 = work.tile([P, V], F32, name="ratio2")
-        nc.vector.tensor_tensor(ratio2[:], inv2[:], num2[:], ALU.mult)
         res2 = work.tile([P, V], F32, name="res2")
-        nc.vector.tensor_scalar(res2[:], ratio2[:], 0.5, 1.0, ALU.mult, ALU.add)
+        nc.vector.scalar_tensor_tensor(res2[:], inv2[:], 0.5, num2[:], ALU.mult, ALU.mult)
         nc.sync.dma_start(out[2 * P : 3 * P, :], res2[:])
         res3 = work.tile([P, V], F32, name="res3")
         nc.vector.scalar_tensor_tensor(res3[:], num3[:], 0.5, inv23[:, 1, :], ALU.mult, ALU.mult)

@@ -22,9 +22,8 @@ PASSES = K // (P * PACK)
 BANK = 512
 GROUPS = BANK // D
 TILES = S // P
-SCALAR_SHARE = (96, 64, 16)
+SCALAR_SHARE = 16
 LAST_PIECES = 4
-TAIL = 32
 REACH = 30.0
 H_BANKS = (0, 1, 3, 1)
 Y_BANKS = ((2, 3), (4, 5), (6, 7), (2, 3))
@@ -34,19 +33,24 @@ def tile_picked_ytop1_top1_p_kernel(tc, x_words, x_scales, w1, e_words, e_scales
     nc = tc.nc
     with ExitStack() as ctx:
         keep = ctx.enter_context(tc.tile_pool(name="keep", bufs=1))
-        work = ctx.enter_context(tc.tile_pool(name="work", bufs=4))
         psum = ctx.enter_context(tc.psum_pool(name="psum", bufs=1))
+
+        def sbuf(shape, dtype, name, takes_over=None):
+            return keep.tile(shape, dtype, name=name, tag=takes_over or name, align_bytes=64)
+
+        def bank(shape, number, name):
+            return psum.tile(shape, F32, name=name, tag="bank%d" % number)
 
         offs_sb = keep.tile([P, S // 16], U16, name="offs_sb")
         neg_sb = keep.tile([P, U // 16], U16, name="neg_sb")
-        xw = [keep.tile([P, T], U32, name="xw%d" % g, align_bytes=64) for g in range(PASSES)]
-        xs = keep.tile([P, T], U8, name="xs", align_bytes=64)
-        ew = keep.tile([P, W], U32, name="ew", align_bytes=64)
-        es = keep.tile([P, W], U8, name="es", align_bytes=64)
+        xw = [sbuf([P, T], U32, "xw%d" % g) for g in range(PASSES)]
+        xs = sbuf([P, T], U8, "xs")
+        ew = sbuf([P, W], U32, "ew")
+        es = sbuf([P, W], U8, "es")
         w_pieces = ((0, 0, H), (1, 0, H // 2), (1, H // 2, H // 2))
-        w_raw = [keep.tile([P, PACK, n], F32, name="w_raw%d" % c, align_bytes=64) for c, (g, first, n) in enumerate(w_pieces)]
-        pos_sb = keep.tile([P, TILES, V], F32, name="pos_sb")
-        ident = keep.tile([P, P], F32, name="ident")
+        w_raw = [sbuf([P, PACK, n], F32, "w_raw%d" % c) for c, (g, first, n) in enumerate(w_pieces)]
+        pos_sb = sbuf([P, TILES, V], F32, "pos_sb")
+        ident = sbuf([P, P], F32, "ident")
 
         nc.gpsimd.memset(es[:].bitcast(I32), 0)
         nc.gpsimd.memset(xs[:].bitcast(I32), 0)
@@ -74,53 +78,51 @@ def tile_picked_ytop1_top1_p_kernel(tc, x_words, x_scales, w1, e_words, e_scales
 
         make_identity(nc, ident[:])
 
-        xg0 = keep.tile([P, S], U32, name="xg0", align_bytes=64)
-        xg1_first = keep.tile([P, P], U32, name="xg1_first", align_bytes=64)
-        xsg = keep.tile([P, S], U8, name="xsg", align_bytes=64)
-        eg = [[keep.tile([P, BANK], U32, name="eg0", align_bytes=64)], []]
-        esg = [keep.tile([P, BANK], U8, name="esg%d" % h, align_bytes=64) for h in range(U // BANK)]
-        wq = {}
-        wsc = [keep.tile([P, H], U8, name="wsc%d" % g, align_bytes=64) for g in range(PASSES)]
+        def gather(dst, table, places, first, count):
+            nc.vector.tensor_copy(dst[:], table[:].indirect(places[:, first // 16 : (first + count) // 16]))
 
-        def neg_cols(h):
-            return neg_sb[:, h * BANK // 16 : (h + 1) * BANK // 16]
+        w_bf = [sbuf([P, PACK * H], BF16, "w_bf%d" % g) for g in range(PASSES)]
+        wsc = [sbuf([P, H], U8, "wsc%d" % g) for g in range(PASSES)]
 
-        w_bf = [keep.tile([P, PACK * H], BF16, name="w_bf%d" % g, align_bytes=64) for g in range(PASSES)]
-
-        def cast_w1(c):
+        def round_w1(c, on_scalar):
             g, first, n = w_pieces[c]
             dst = w_bf[g][:].rearrange("p (t m j) -> p m t j", t=PACK, j=PACK)[:, first // PACK : (first + n) // PACK]
             src = w_raw[c][:].rearrange("p j (m t) -> p m t j", t=PACK)
-            m_split = SCALAR_SHARE[c]
-            nc.scalar.activation(dst[:, :m_split], src[:, :m_split], ACT.Copy)
-            if m_split < n // PACK:
-                nc.vector.tensor_copy(dst[:, m_split:], src[:, m_split:])
+            nc.scalar.activation(dst[:, :on_scalar], src[:, :on_scalar], ACT.Copy)
+            if on_scalar < n // PACK:
+                nc.vector.tensor_copy(dst[:, on_scalar:], src[:, on_scalar:])
 
-        def quantize_w1(g, pieces):
+        def quantize_w1(g, pieces, takes_over=None):
+            codes = sbuf([P, H], U32, "wq%d" % g, takes_over)
             n = H // pieces
-            wq[g] = keep.tile([P, H], U32, name="wq%d" % g, tag="xw0" if g == 0 else "wq1", align_bytes=64)
             for c in range(pieces):
                 cols = slice(n * c, n * (c + 1))
-                nc.vector.quantize_mx(out=wq[g][:, cols].bitcast(FP8X4), scales=wsc[g][:, cols], in_=w_bf[g][:, PACK * n * c : PACK * n * (c + 1)])
+                nc.vector.quantize_mx(out=codes[:, cols].bitcast(FP8X4), scales=wsc[g][:, cols], in_=w_bf[g][:, PACK * n * c : PACK * n * (c + 1)])
+            return codes
 
+        esg = [sbuf([P, BANK], U8, "esg%d" % h) for h in range(U // BANK)]
         for h in range(U // BANK):
-            nc.vector.tensor_copy(esg[h][:], es[:].indirect(neg_cols(h)))
-        cast_w1(0)
-        nc.vector.tensor_copy(xsg[:], xs[:].indirect(offs_sb[:]))
-        nc.vector.tensor_copy(xg0[:], xw[0][:].indirect(offs_sb[:]))
-        quantize_w1(0, 1)
-        cast_w1(1)
-        cast_w1(2)
-        quantize_w1(1, 2)
-        nc.vector.tensor_copy(xg1_first[:], xw[1][:].indirect(offs_sb[:, : P // 16]))
-        xg1_rest = keep.tile([P, S - P], U32, name="xg1_rest", align_bytes=64)
-        nc.vector.tensor_copy(xg1_rest[:], xw[1][:].indirect(offs_sb[:, P // 16 :]))
-        nc.vector.tensor_copy(eg[0][0][:], ew[:].indirect(neg_cols(0)))
+            gather(esg[h], es, neg_sb, BANK * h, BANK)
+        round_w1(0, H // PACK)
+        xsg = sbuf([P, S], U8, "xsg")
+        gather(xsg, xs, offs_sb, 0, S)
+        xg0 = sbuf([P, S], U32, "xg0")
+        gather(xg0, xw[0], offs_sb, 0, S)
+        wq = [quantize_w1(0, 1, "xw0")]
+        round_w1(1, H // (2 * PACK))
+        round_w1(2, SCALAR_SHARE)
+        wq.append(quantize_w1(1, 2))
+        xg1_first = sbuf([P, P], U32, "xg1_first")
+        gather(xg1_first, xw[1], offs_sb, 0, P)
+        xg1_rest = sbuf([P, S - P], U32, "xg1_rest")
+        gather(xg1_rest, xw[1], offs_sb, P, S - P)
+        eg = [sbuf([P, BANK], U32, "eg0")]
+        gather(eg[0], ew, neg_sb, 0, BANK)
 
         def hidden(i):
             tok = slice(P * i, P * (i + 1))
             x_codes = [xg0[:, tok], xg1_first[:] if i == 0 else xg1_rest[:, P * (i - 1) : P * i]]
-            h_ps = psum.tile([P, PACK, P], F32, name="h_ps", tag="bank%d" % H_BANKS[i])
+            h_ps = bank([P, PACK, P], H_BANKS[i], "h_ps")
             for j in range(PACK):
                 for g in range(PASSES):
                     nc.tensor.matmul_mx(
@@ -132,227 +134,201 @@ def tile_picked_ytop1_top1_p_kernel(tc, x_words, x_scales, w1, e_words, e_scales
                         start=(g == 0),
                         stop=(g == PASSES - 1),
                     )
-            h_bf = keep.tile([P, P * PACK], BF16, name="h_bf", tag="h_bf%d" % i, align_bytes=64)
+            h_bf = sbuf([P, P * PACK], BF16, "h_bf%d" % i)
             nc.scalar.activation(h_bf[:].rearrange("p (n j) -> p n j", j=PACK), h_ps[:].rearrange("p j n -> p n j"), ACT.Copy)
-            hq = keep.tile([P, P], U32, name="hq%d" % i, align_bytes=64)
-            hs = keep.tile([P, P], U8, name="hs%d" % i, align_bytes=64)
+            hq = sbuf([P, P], U32, "hq%d" % i)
+            hs = sbuf([P, P], U8, "hs%d" % i)
             nc.vector.quantize_mx(out=hq[:].bitcast(FP8X4), scales=hs[:], in_=h_bf[:])
             return hq, hs
 
+        y = {}
+
         def scores(i, h):
             hq, hs = quantised[i]
-            y_ps = psum.tile([P, BANK], F32, name="y_ps", tag="bank%d" % Y_BANKS[i][h])
-            col = 0
-            for words in eg[h]:
-                n = words.shape[1]
-                nc.tensor.matmul_mx(
-                    out=y_ps[:, col : col + n], lhsT=hq[:].bitcast(FP8X4), lhsT_scale=hs[:],
-                    rhs=words[:].bitcast(FP8X4), rhs_scale=esg[h][:, col : col + n], start=True, stop=True,
-                )
-                col += n
-            return y_ps
+            y[i, h] = bank([P, BANK], Y_BANKS[i][h], "y_ps")
+            nc.tensor.matmul_mx(
+                out=y[i, h][:], lhsT=hq[:].bitcast(FP8X4), lhsT_scale=hs[:],
+                rhs=eg[h][:].bitcast(FP8X4), rhs_scale=esg[h][:], start=True, stop=True,
+            )
 
-        def sum_over_group(acc, terms):
-            for d in range(D):
+        def add_turned(acc, terms, members):
+            for d in members:
                 nc.tensor.matmul(acc, lhsT=terms[:, d, :], rhs=ident[:], is_transpose=True, start=(d == 0), stop=(d == D - 1))
 
         halves = [slice(GROUPS * h, GROUPS * (h + 1)) for h in range(U // BANK)]
+        member_halves = [slice(D // 2 * c, D // 2 * (c + 1)) for c in range(2)]
         wide = [P, D, GROUPS]
+        args = [sbuf([P, 2 * D, V], F32, "args%d" % i) for i in range(TILES)]
+        th = [sbuf([P, 2 * D, V], F32, "th%d" % i) for i in range(TILES)]
+        ex = [sbuf([P, D, V], F32, "ex%d" % i) for i in range(TILES)]
+        z = [sbuf([P, D, V], F32, "z%d" % i) for i in range(TILES)]
+        top = [sbuf([P, V], F32, "top%d" % i) for i in range(TILES - 1)]
+        below = [sbuf([P, D, V], F32, "below%d" % i) for i in range(TILES - 1)]
+        both = [sbuf([P, D, V], F32, "both%d" % i) for i in range(TILES - 1)]
 
-        def tiles_of(i):
-            top = work.tile([P, V], F32, name="top")
-            below = work.tile([P, D, V], F32, name="below")
-            ex = keep.tile([P, D, V], F32, name="ex", tag="ex%d" % i)
-            args = keep.tile([P, 2 * D, V], F32, name="args", tag="args%d" % i)
-            th = work.tile([P, 2 * D, V], F32, name="th")
-            both = work.tile([P, D, V], F32, name="both")
-            z = work.tile([P, D, V], F32, name="z")
-            return {"top": top, "below": below, "ex": ex, "args": args, "th": th, "both": both, "z": z}
+        def by_member(i, h):
+            return y[i, h][:].rearrange("p (v d) -> p d v", d=D)
 
-        def by_member(y_ps):
-            return y_ps[:].rearrange("p (v d) -> p d v", d=D)
+        def over_members(per_group):
+            return per_group.unsqueeze(1).to_broadcast(wide)
 
-        def minus_pos(i, t, y_ps, vs):
-            nc.vector.tensor_tensor(t["args"][:, :D, vs], by_member(y_ps), pos_sb[:, i, vs].unsqueeze(1).to_broadcast(wide), ALU.subtract)
+        def largest(dst, i, h):
+            nc.vector.tensor_reduce(dst, y[i, h][:].rearrange("p (v d) -> p v d", d=D), mybir.AxisListType.X, ALU.max)
 
-        def squares(t, y_ps, vs):
-            nc.scalar.activation(t["args"][:, D:, vs], by_member(y_ps), ACT.Square)
+        def minus_pos(i, h):
+            nc.vector.tensor_tensor(args[i][:, :D, halves[h]], by_member(i, h), over_members(pos_sb[:, i, halves[h]]), ALU.subtract)
 
-        def minus_top(t, y_ps, vs):
-            nc.vector.tensor_reduce(t["top"][:, vs], y_ps[:].rearrange("p (v d) -> p v d", d=D), mybir.AxisListType.X, ALU.max)
-            nc.vector.tensor_tensor(t["below"][:, :, vs], by_member(y_ps), t["top"][:, vs].unsqueeze(1).to_broadcast(wide), ALU.subtract)
+        def minus_top(i, h):
+            largest(top[i][:, halves[h]], i, h)
+            nc.vector.tensor_tensor(below[i][:, :, halves[h]], by_member(i, h), over_members(top[i][:, halves[h]]), ALU.subtract)
 
-        def exps(t, vs):
-            nc.scalar.activation(t["ex"][:, :, vs], t["below"][:, :, vs], ACT.Exp)
+        def squares(i, h):
+            nc.scalar.activation(args[i][:, D:, halves[h]], by_member(i, h), ACT.Square)
 
-        def gates(t, vs):
-            nc.scalar.activation(t["th"][:, :, vs], t["args"][:, :, vs], ACT.Tanh, scale=0.5)
+        def exps(i, h):
+            nc.scalar.activation(ex[i][:, :, halves[h]], below[i][:, :, halves[h]], ACT.Exp)
 
-        def add_gates(engine, t, vs):
-            engine.tensor_tensor(t["both"][:, :, vs], t["th"][:, :D, vs], t["th"][:, D:, vs], ALU.add)
+        def gates(i, h):
+            nc.scalar.activation(th[i][:, :, halves[h]], args[i][:, :, halves[h]], ACT.Tanh, scale=0.5)
 
-        def weigh(t, vs, engine=nc.gpsimd):
-            engine.tensor_tensor(t["z"][:, :, vs], t["both"][:, :, vs], t["ex"][:, :, vs], ALU.mult)
+        def add_gates(engine, i, h):
+            engine.tensor_tensor(both[i][:, :, halves[h]], th[i][:, :D, halves[h]], th[i][:, D:, halves[h]], ALU.add)
 
-        def split(vs):
-            return [slice(a, a + TAIL) for a in range(vs.start, vs.stop, TAIL)]
-
-        def inverses(totals, first_tag, inv_tag, kept, later_totals):
-            first = keep.tile([P, P], F32, name="first", tag=first_tag)
-            nc.vector.tensor_copy(first[:], totals[:, 0, :])
-            prod = work.tile([P, P], F32, name="prod")
-            nc.vector.tensor_tensor(prod[:], totals[:, 1, :], first[:], ALU.mult)
-            inv_prod = work.tile([P, P], F32, name="inv_prod")
-            nc.vector.reciprocal(inv_prod[:], prod[:])
-            nc.vector.tensor_copy(kept[:], later_totals[:, 0, :])
-            inv = keep.tile([P, 2, P], F32, name="inv", tag=inv_tag)
-            nc.vector.tensor_tensor(inv[:], totals[:, :2, :], inv_prod[:].unsqueeze(1).to_broadcast([P, 2, P]), ALU.mult)
-            return inv
+        def weigh(i, h):
+            nc.gpsimd.tensor_tensor(z[i][:, :, halves[h]], both[i][:, :, halves[h]], ex[i][:, :, halves[h]], ALU.mult)
 
         quantised = [hidden(0)]
-        eg[1].append(keep.tile([P, BANK], U32, name="eg1", tag="h_bf0", align_bytes=64))
-        banks = {(0, 0): scores(0, 0)}
-        nc.vector.tensor_copy(eg[1][0][:], ew[:].indirect(neg_cols(1)))
-        ts = [tiles_of(i) for i in range(TILES)]
-        t0, t1, t2, t3 = ts
-        order = [(i, h) for i in range(TILES) for h in range(2)]
-
-        def gate_sum(i, h, pieces):
-            for piece in pieces:
-                gates(ts[i], piece)
-                add_gates(nc.gpsimd, ts[i], piece)
-
-        def square(k):
-            i, h = order[k]
-            squares(ts[i], banks[i, h], halves[h])
-
-        square(0)
-        minus_pos(0, t0, banks[0, 0], halves[0])
+        scores(0, 0)
+        eg.append(sbuf([P, BANK], U32, "eg1", "h_bf0"))
+        gather(eg[1], ew, neg_sb, BANK, BANK)
+        squares(0, 0)
+        minus_pos(0, 0)
         quantised.extend(hidden(i) for i in range(1, TILES))
-        banks[0, 1] = scores(0, 1)
-        gate_sum(0, 0, split(halves[0]))
-        for i in range(1, TILES - 1):
+        scores(0, 1)
+        gates(0, 0)
+        add_gates(nc.gpsimd, 0, 0)
+        for i in (1, 2):
             for h in range(2):
-                banks[i, h] = scores(i, h)
-        square(1)
-        minus_top(t0, banks[0, 0], halves[0])
-        exps(t0, halves[0])
-        weigh(t0, halves[0])
-        pos_turned = psum.tile([P, P], F32, name="pos_turned", tag="bank1")
-        nc.tensor.transpose(pos_turned[:], pos_sb[:, 3, :], ident[:])
-        pos_turned_sb = keep.tile([P, P], F32, name="pos_turned_sb")
-        nc.scalar.activation(pos_turned_sb[:], pos_turned[:], ACT.Copy, bias=REACH)
-        raised = psum.tile([P, P], F32, name="raised", tag="bank1")
-        nc.tensor.transpose(raised[:], pos_turned_sb[:], ident[:])
-        for k in range(1, 4):
-            i, h = order[k]
-            t, vs = ts[i], halves[h]
-            minus_pos(i, t, banks[i, h], vs)
-            square(k + 1)
-            minus_top(t, banks[i, h], vs)
-            gate_sum(i, h, [vs])
-            exps(t, vs)
-            weigh(t, vs)
-            if i == 0:
-                for h in range(2):
-                    banks[3, h] = scores(3, h)
-                totals01 = psum.tile([P, 2, P], F32, name="totals01", tag="bank0")
-                sum_over_group(totals01[:, 0, :], t0["ex"])
+                scores(i, h)
+        squares(0, 1)
+        minus_top(0, 0)
+        exps(0, 0)
+        weigh(0, 0)
 
-        bounds = keep.tile([P, 2, V], F32, name="bounds")
-        shift = keep.tile([P, V], F32, name="shift")
-        for h, vs in enumerate(halves):
-            nc.vector.tensor_reduce(bounds[:, 0, vs], banks[3, h][:].rearrange("p (v d) -> p v d", d=D), mybir.AxisListType.X, ALU.max)
+        pos_turned = bank([P, P], 1, "pos_turned")
+        nc.tensor.transpose(pos_turned[:], pos_sb[:, 3, :], ident[:])
+        pos_turned_sb = sbuf([P, P], F32, "pos_turned_sb")
+        nc.scalar.activation(pos_turned_sb[:], pos_turned[:], ACT.Copy, bias=REACH)
+        raised = bank([P, P], 1, "raised")
+        nc.tensor.transpose(raised[:], pos_turned_sb[:], ident[:])
+
+        for (i, h), ahead in (((0, 1), (1, 0)), ((1, 0), (1, 1)), ((1, 1), (2, 0))):
+            minus_pos(i, h)
+            squares(*ahead)
+            minus_top(i, h)
+            gates(i, h)
+            add_gates(nc.gpsimd, i, h)
+            exps(i, h)
+            weigh(i, h)
+            if i == 0:
+                scores(3, 0)
+                scores(3, 1)
+                totals01 = bank([P, 2, P], 0, "totals01")
+                add_turned(totals01[:, 0, :], ex[0], range(D))
+
+        bounds = sbuf([P, 2, V], F32, "bounds")
+        shift = sbuf([P, V], F32, "shift")
+        for h in range(2):
+            largest(bounds[:, 0, halves[h]], 3, h)
         nc.vector.scalar_tensor_tensor(bounds[:, 1, :], bounds[:, 0, :], 2 * REACH, raised[:], ALU.add, ALU.min)
         nc.vector.tensor_reduce(shift[:], bounds[:].rearrange("p r v -> p v r"), mybir.AxisListType.X, ALU.max)
-        for h, vs in enumerate(halves):
-            nc.vector.scalar_tensor_tensor(t3["args"][:, :D, vs], by_member(banks[3, h]), REACH, shift[:, vs].unsqueeze(1).to_broadcast(wide), ALU.add, ALU.subtract)
-        minus_pos(2, t2, banks[2, 0], halves[0])
-        sum_over_group(totals01[:, 1, :], t1["ex"])
-        gate_sum(2, 0, [halves[0]])
-        square(5)
-        square(6)
-        square(7)
-        for c in range(2):
-            turned = psum.tile([P, D // 2, P], F32, name="turned", tag="bank%d" % (4 + c))
+        for h in range(2):
+            nc.vector.scalar_tensor_tensor(args[3][:, :D, halves[h]], by_member(3, h), REACH, over_members(shift[:, halves[h]]), ALU.add, ALU.subtract)
+        minus_pos(2, 0)
+        add_turned(totals01[:, 1, :], ex[1], range(D))
+        gates(2, 0)
+        add_gates(nc.gpsimd, 2, 0)
+        squares(2, 1)
+        squares(3, 0)
+        squares(3, 1)
+        for c, members in enumerate(member_halves):
+            turned = bank([P, D // 2, P], 4 + c, "turned")
             for d in range(D // 2):
-                nc.tensor.transpose(turned[:, d, :], t3["args"][:, D // 2 * c + d, :], ident[:])
-            nc.scalar.activation(t3["ex"][:, D // 2 * c : D // 2 * (c + 1), :], turned[:], ACT.Exp)
+                nc.tensor.transpose(turned[:, d, :], args[3][:, members.start + d, :], ident[:])
+            nc.scalar.activation(ex[3][:, members, :], turned[:], ACT.Exp)
 
-        minus_pos(2, t2, banks[2, 1], halves[1])
-        gates(t2, halves[1])
-        for h, vs in enumerate(halves):
-            minus_top(t2, banks[2, h], vs)
-        totals23 = psum.tile([P, 2, P], F32, name="totals23", tag="bank6")
-        sum_over_group(totals23[:, 0, :], t3["ex"])
-        first23 = keep.tile([P, P], F32, name="first23")
-        inv01 = inverses(totals01, "first01", "inv01", first23, totals23)
-        add_gates(nc.vector, t2, halves[1])
-        for c in range(2):
-            ds = slice(D // 2 * c, D // 2 * (c + 1))
-            nc.scalar.activation(t2["ex"][:, ds, :], t2["below"][:, ds, :], ACT.Exp)
-        nc.vector.scalar_tensor_tensor(t2["z"][:], t2["both"][:], 2.0, t2["ex"][:], ALU.add, ALU.mult)
-        sum_over_group(totals23[:, 1, :], t2["ex"])
+        minus_pos(2, 1)
+        gates(2, 1)
+        minus_top(2, 0)
+        minus_top(2, 1)
+        totals23 = bank([P, 2, P], 6, "totals23")
+        add_turned(totals23[:, 0, :], ex[3], range(D))
 
-        nums = []
-        for a in range(2):
-            num = psum.tile([P, P], F32, name="num", tag="bank%d" % (1, 7)[a])
-            sum_over_group(num[:], ts[a]["z"])
-            ratio = work.tile([P, P], F32, name="ratio")
-            nc.vector.tensor_tensor(ratio[:], num[:], inv01[:, 1 - a, :], ALU.mult)
-            nums.append(ratio)
-        back = psum.tile([P, 2, P], F32, name="back", tag="bank1")
-        for a in range(2):
-            nc.tensor.transpose(back[:, a, :], nums[a][:], ident[:])
-        prod23 = keep.tile([P, P], F32, name="prod23")
-        nc.vector.tensor_tensor(prod23[:], totals23[:, 1, :], first23[:], ALU.mult)
-        inv_prod23 = keep.tile([P, P], F32, name="inv_prod23")
+        total0 = sbuf([P, P], F32, "total0")
+        nc.vector.tensor_copy(total0[:], totals01[:, 0, :])
+        prod01 = sbuf([P, P], F32, "prod01")
+        nc.vector.tensor_tensor(prod01[:], totals01[:, 1, :], total0[:], ALU.mult)
+        inv_prod01 = sbuf([P, P], F32, "inv_prod01")
+        nc.vector.reciprocal(inv_prod01[:], prod01[:])
+        total3 = sbuf([P, P], F32, "total3")
+        nc.vector.tensor_copy(total3[:], totals23[:, 0, :])
+        inv10 = sbuf([P, 2, P], F32, "inv10")
+        nc.vector.tensor_tensor(inv10[:], totals01[:], inv_prod01[:].unsqueeze(1).to_broadcast([P, 2, P]), ALU.mult)
+
+        add_gates(nc.vector, 2, 1)
+        for members in member_halves:
+            nc.scalar.activation(ex[2][:, members, :], below[2][:, members, :], ACT.Exp)
+        nc.vector.scalar_tensor_tensor(z[2][:], both[2][:], 2.0, ex[2][:], ALU.add, ALU.mult)
+        add_turned(totals23[:, 1, :], ex[2], range(D))
+
+        ratios = []
+        for i, number in ((0, 1), (1, 7)):
+            num = bank([P, P], number, "num")
+            add_turned(num[:], z[i], range(D))
+            ratios.append(sbuf([P, P], F32, "ratio%d" % i))
+            nc.vector.tensor_tensor(ratios[i][:], num[:], inv10[:, 1 - i, :], ALU.mult)
+        back = bank([P, 2, P], 1, "back")
+        for i in range(2):
+            nc.tensor.transpose(back[:, i, :], ratios[i][:], ident[:])
+        prod23 = sbuf([P, P], F32, "prod23")
+        nc.vector.tensor_tensor(prod23[:], totals23[:, 1, :], total3[:], ALU.mult)
+        inv_prod23 = sbuf([P, P], F32, "inv_prod23")
         nc.vector.reciprocal(inv_prod23[:], prod23[:])
-        inv23 = keep.tile([P, 2, P], F32, name="inv23")
-        nc.vector.tensor_tensor(inv23[:], totals23[:], inv_prod23[:].unsqueeze(1).to_broadcast([P, 2, P]), ALU.mult)
+        inv2_turned = sbuf([P, P], F32, "inv2_turned")
+        nc.vector.tensor_tensor(inv2_turned[:], totals23[:, 0, :], inv_prod23[:], ALU.mult)
 
         n = D // LAST_PIECES
-        num3 = psum.tile([P, P], F32, name="num3", tag="bank0")
-        args3 = t3["args"][:].rearrange("p (k d) v -> p k d v", k=2)
-        th3 = t3["th"][:].rearrange("p (k d) v -> p k d v", k=2)
-        part = work.tile([P, D // 2, V], F32, name="part")
-
-        def fold(step):
-            if step == 0:
-                nc.gpsimd.tensor_tensor(part[:], t2["z"][:, : D // 2, :], t2["z"][:, D // 2 :, :], ALU.add)
-            else:
-                m = D // 2 >> step
-                nc.gpsimd.tensor_tensor(part[:, :m, :], part[:, :m, :], part[:, m : 2 * m, :], ALU.add)
-
-        sums = []
-        for c in range(LAST_PIECES):
-            ds = slice(n * c, n * (c + 1))
-            nc.scalar.activation(th3[:, :, ds, :], args3[:, :, ds, :], ACT.Tanh, scale=0.5)
-            gate_sums = psum.tile([P, n, P], F32, name="gate_sums", tag="bank%d" % (4, 5, 2, 3)[c])
+        pieces = [slice(n * c, n * (c + 1)) for c in range(LAST_PIECES)]
+        args3 = args[3][:].rearrange("p (k d) v -> p k d v", k=2)
+        th3 = th[3][:].rearrange("p (k d) v -> p k d v", k=2)
+        gate_sums = []
+        for members, number in zip(pieces, (4, 5, 2, 3)):
+            nc.scalar.activation(th3[:, :, members, :], args3[:, :, members, :], ACT.Tanh, scale=0.5)
+            gate_sums.append(bank([P, n, P], number, "gate_sums"))
             for d in range(n):
                 for k in range(2):
-                    nc.tensor.matmul(gate_sums[:, d, :], lhsT=th3[:, k, n * c + d, :], rhs=ident[:], is_transpose=True, start=(k == 0), stop=(k == 1))
-            sums.append(gate_sums)
-        res = work.tile([P, 2, V], F32, name="res")
-        nc.scalar.activation(res[:], back[:], ACT.Copy, bias=1.0, scale=0.5)
-        nc.sync.dma_start(out[: 2 * P, :].rearrange("(a p) v -> p a v", p=P), res[:])
-        for step in range(1):
-            fold(step)
-        for c in range(LAST_PIECES):
-            ds = slice(n * c, n * (c + 1))
-            nc.vector.scalar_tensor_tensor(t3["z"][:, ds, :], sums[c][:], 2.0, t3["ex"][:, ds, :], ALU.add, ALU.mult)
-            for d in range(n * c, n * (c + 1)):
-                nc.tensor.matmul(num3[:], lhsT=t3["z"][:, d, :], rhs=ident[:], is_transpose=True, start=(d == 0), stop=(d == D - 1))
+                    nc.tensor.matmul(gate_sums[-1][:, d, :], lhsT=th3[:, k, members.start + d, :], rhs=ident[:], is_transpose=True, start=(k == 0), stop=(k == 1))
+        res01 = sbuf([P, 2, V], F32, "res01")
+        nc.scalar.activation(res01[:], back[:], ACT.Copy, bias=1.0, scale=0.5)
+        nc.sync.dma_start(out[: 2 * P, :].rearrange("(a p) v -> p a v", p=P), res01[:])
+        fours = sbuf([P, D // 2, V], F32, "fours")
+        nc.gpsimd.tensor_tensor(fours[:], z[2][:, : D // 2, :], z[2][:, D // 2 :, :], ALU.add)
+        num3 = bank([P, P], 0, "num3")
+        for members, sums in zip(pieces, gate_sums):
+            nc.vector.scalar_tensor_tensor(z[3][:, members, :], sums[:], 2.0, ex[3][:, members, :], ALU.add, ALU.mult)
+            add_turned(num3[:], z[3], range(members.start, members.stop))
 
-        inv2 = psum.tile([P, P], F32, name="inv2", tag="bank4")
-        nc.tensor.transpose(inv2[:], inv23[:, 0, :], ident[:])
-        half = keep.tile([P, 2, V], F32, name="half")
-        nc.gpsimd.tensor_tensor(half[:], part[:, :2, :], part[:, 2:, :], ALU.add)
-        num2 = work.tile([P, V], F32, name="num2")
-        nc.gpsimd.tensor_tensor(num2[:], half[:, 0, :], half[:, 1, :], ALU.add)
-        res2 = work.tile([P, V], F32, name="res2")
+        inv2 = bank([P, P], 4, "inv2")
+        nc.tensor.transpose(inv2[:], inv2_turned[:], ident[:])
+        twos = sbuf([P, 2, V], F32, "twos")
+        nc.gpsimd.tensor_tensor(twos[:], fours[:, :2, :], fours[:, 2:, :], ALU.add)
+        num2 = sbuf([P, V], F32, "num2")
+        nc.gpsimd.tensor_tensor(num2[:], twos[:, 0, :], twos[:, 1, :], ALU.add)
+        res2 = sbuf([P, V], F32, "res2")
         nc.vector.scalar_tensor_tensor(res2[:], inv2[:], 0.5, num2[:], ALU.mult, ALU.mult)
         nc.sync.dma_start(out[2 * P : 3 * P, :], res2[:])
-        res3 = work.tile([P, V], F32, name="res3")
-        nc.vector.scalar_tensor_tensor(res3[:], num3[:], 0.5, inv23[:, 1, :], ALU.mult, ALU.mult)
+        inv3 = sbuf([P, P], F32, "inv3")
+        nc.vector.tensor_tensor(inv3[:], totals23[:, 1, :], inv_prod23[:], ALU.mult)
+        res3 = sbuf([P, V], F32, "res3")
+        nc.vector.scalar_tensor_tensor(res3[:], num3[:], 0.5, inv3[:], ALU.mult, ALU.mult)
         nc.sync.dma_start(out[3 * P :, :], res3[:])

@@ -58,15 +58,17 @@ def tile_picked_ytop1_top1_p_kernel(tc, x_words, x_scales, w1, e_words, e_scales
         def load_words(dst, words):
             nc.sync.dma_start(dst[:].bitcast(I32), words.rearrange("p n t -> p (n t)").bitcast(I32))
 
-        def load_w1(c):
+        def load_w1(c, rows=slice(0, PACK)):
             g, first, n = w_pieces[c]
-            nc.sync.dma_start(w_raw[c][:], w1[512 * g : 512 * (g + 1), first : first + n].rearrange("(p j) c -> p j c", j=PACK))
+            src = w1[512 * g : 512 * (g + 1), first : first + n].rearrange("(p j) c -> p j c", j=PACK)
+            nc.sync.dma_start(w_raw[c][:, rows, :], src[:, rows, :])
 
         nc.sync.dma_start(offs_sb[:], offs)
         nc.sync.dma_start(neg_sb[:], neg)
+        load_w1(0, slice(0, 1))
         for q in range(4):
             nc.sync.dma_start(es[32 * q : 32 * q + 4, :].bitcast(I32), e_scales[0, 4 * q : 4 * q + 4, :].bitcast(I32))
-        load_w1(0)
+        load_w1(0, slice(1, PACK))
         for q in range(4):
             nc.sync.dma_start(xs[32 * q : 32 * q + 4 * PASSES, :].bitcast(I32), x_scales[:, 4 * q : 4 * q + 4, :].bitcast(I32))
         load_words(xw[0], x_words[0])
@@ -77,11 +79,15 @@ def tile_picked_ytop1_top1_p_kernel(tc, x_words, x_scales, w1, e_words, e_scales
         nc.sync.dma_start(pos_sb[:], pos.rearrange("(a p) v -> p a v", p=P))
 
         make_identity(nc, ident[:])
+        seed = sbuf([P, 1], F32, "seed")
+        nc.vector.memset(seed[:], REACH)
+        reach = sbuf([P, 1], F32, "reach")
+        nc.scalar.activation(reach[:], seed[:], ACT.Copy)
 
         def gather(dst, table, places, first, count):
             nc.vector.tensor_copy(dst[:], table[:].indirect(places[:, first // 16 : (first + count) // 16]))
 
-        w_bf = [sbuf([P, PACK * H], BF16, "w_bf%d" % g) for g in range(PASSES)]
+        w_bf = [sbuf([P, PACK * H], BF16, "w_bf%d" % g, earlier) for g, earlier in enumerate(("seed", None))]
         wsc = [sbuf([P, H], U8, "wsc%d" % g) for g in range(PASSES)]
 
         def round_w1(c, on_scalar):
@@ -218,7 +224,7 @@ def tile_picked_ytop1_top1_p_kernel(tc, x_words, x_scales, w1, e_words, e_scales
         pos_turned = bank([P, P], 1, "pos_turned")
         nc.tensor.transpose(pos_turned[:], pos_sb[:, 3, :], ident[:])
         pos_turned_sb = sbuf([P, P], F32, "pos_turned_sb")
-        nc.scalar.activation(pos_turned_sb[:], pos_turned[:], ACT.Copy, bias=REACH)
+        nc.scalar.activation(pos_turned_sb[:], pos_turned[:], ACT.Identity, bias=reach[:])
         raised = bank([P, P], 1, "raised")
         nc.tensor.transpose(raised[:], pos_turned_sb[:], ident[:])
 

@@ -1,3 +1,4 @@
+import math
 from contextlib import ExitStack
 
 import concourse.mybir as mybir
@@ -15,6 +16,7 @@ U8 = mybir.dt.uint8
 FP8X4 = mybir.dt.float8_e4m3fn_x4
 ALU = mybir.AluOpType
 ACT = mybir.ActivationFunctionType
+AXIS_X = mybir.AxisListType.X
 
 P = 128
 PACK = 4
@@ -22,11 +24,15 @@ PASSES = K // (P * PACK)
 BANK = 512
 GROUPS = BANK // D
 TILES = S // P
+UNITS = 4
 SCALAR_SHARE = 16
+REACH = 18.0
+TAIL = 36.0
+LIFT = 2.0 ** 52
+E_PLANE = 8
 LAST_PIECES = 4
-REACH = 30.0
-H_BANKS = (0, 1, 3, 1)
-Y_BANKS = ((2, 3), (4, 5), (6, 7), (2, 3))
+H_BANKS = (0, 1, 2, 3)
+Y_BANKS = ((4, 5), (6, 7), (0, 1), (2, 3))
 
 
 def tile_picked_ytop1_top1_p_kernel(tc, x_words, x_scales, w1, e_words, e_scales, pos, offs, neg, out):
@@ -49,7 +55,7 @@ def tile_picked_ytop1_top1_p_kernel(tc, x_words, x_scales, w1, e_words, e_scales
         es = sbuf([P, W], U8, "es")
         w_pieces = ((0, 0, H), (1, 0, H // 2), (1, H // 2, H // 2))
         w_raw = [sbuf([P, PACK, n], F32, "w_raw%d" % c) for c, (g, first, n) in enumerate(w_pieces)]
-        pos_sb = sbuf([P, TILES, V], F32, "pos_sb")
+        pos_sb = [sbuf([P, TILES, GROUPS], F32, "pos_sb%d" % h) for h in range(2)]
         ident = sbuf([P, P], F32, "ident")
 
         nc.gpsimd.memset(es[:].bitcast(I32), 0)
@@ -67,7 +73,7 @@ def tile_picked_ytop1_top1_p_kernel(tc, x_words, x_scales, w1, e_words, e_scales
         nc.sync.dma_start(neg_sb[:], neg)
         load_w1(0, slice(0, 1))
         for q in range(4):
-            nc.sync.dma_start(es[32 * q : 32 * q + 4, :].bitcast(I32), e_scales[0, 4 * q : 4 * q + 4, :].bitcast(I32))
+            nc.sync.dma_start(es[32 * q + E_PLANE : 32 * q + E_PLANE + 4, :].bitcast(I32), e_scales[0, 4 * q : 4 * q + 4, :].bitcast(I32))
         load_w1(0, slice(1, PACK))
         for q in range(4):
             nc.sync.dma_start(xs[32 * q : 32 * q + 4 * PASSES, :].bitcast(I32), x_scales[:, 4 * q : 4 * q + 4, :].bitcast(I32))
@@ -76,18 +82,21 @@ def tile_picked_ytop1_top1_p_kernel(tc, x_words, x_scales, w1, e_words, e_scales
         load_w1(2)
         load_words(xw[1], x_words[1])
         load_words(ew, e_words[0])
-        nc.sync.dma_start(pos_sb[:], pos.rearrange("(a p) v -> p a v", p=P))
+        for h in range(2):
+            nc.sync.dma_start(pos_sb[h][:], pos[:, GROUPS * h : GROUPS * (h + 1)].rearrange("(a p) v -> p a v", p=P))
 
         make_identity(nc, ident[:])
-        seed = sbuf([P, 1], F32, "seed")
-        nc.vector.memset(seed[:], REACH)
-        reach = sbuf([P, 1], F32, "reach")
-        nc.scalar.activation(reach[:], seed[:], ACT.Copy)
+        minus_tail = sbuf([P, 1], F32, "minus_tail")
+        nc.vector.memset(minus_tail[:], -TAIL)
+        tiny = sbuf([P, 1], F32, "tiny")
+        nc.scalar.activation(tiny[:], minus_tail[:], ACT.Sigmoid)
+        minus_tiny = sbuf([P, 1], F32, "minus_tiny")
+        nc.vector.tensor_scalar(minus_tiny[:], tiny[:], -1.0, None, ALU.mult)
 
         def gather(dst, table, places, first, count):
             nc.vector.tensor_copy(dst[:], table[:].indirect(places[:, first // 16 : (first + count) // 16]))
 
-        w_bf = [sbuf([P, PACK * H], BF16, "w_bf%d" % g, earlier) for g, earlier in enumerate(("seed", None))]
+        w_bf = [sbuf([P, PACK * H], BF16, "w_bf%d" % g, earlier) for g, earlier in enumerate(("tiny", None))]
         wsc = [sbuf([P, H], U8, "wsc%d" % g) for g in range(PASSES)]
 
         def round_w1(c, on_scalar):
@@ -106,8 +115,22 @@ def tile_picked_ytop1_top1_p_kernel(tc, x_words, x_scales, w1, e_words, e_scales
                 nc.vector.quantize_mx(out=codes[:, cols].bitcast(FP8X4), scales=wsc[g][:, cols], in_=w_bf[g][:, PACK * n * c : PACK * n * (c + 1)])
             return codes
 
-        esg = [sbuf([P, BANK], U8, "esg%d" % h) for h in range(U // BANK)]
-        for h in range(U // BANK):
+        h_ps = [bank([P, PACK, P], H_BANKS[i], "h_ps%d" % i) for i in range(TILES)]
+
+        def hidden_pass(i, g, x_codes):
+            for j in range(PACK):
+                nc.tensor.matmul_mx(
+                    out=h_ps[i][:, j, :],
+                    lhsT=wq[g][:, P * j : P * (j + 1)].bitcast(FP8X4),
+                    lhsT_scale=wsc[g][:, P * j : P * (j + 1)],
+                    rhs=x_codes.bitcast(FP8X4),
+                    rhs_scale=xsg[4 * g : P, P * i : P * (i + 1)],
+                    start=(g == 0 and j == 0),
+                    stop=(g == PASSES - 1 and j == PACK - 1),
+                )
+
+        esg = [sbuf([P, BANK], U8, "esg%d" % h) for h in range(2)]
+        for h in range(2):
             gather(esg[h], es, neg_sb, BANK * h, BANK)
         round_w1(0, H // PACK)
         xsg = sbuf([P, S], U8, "xsg")
@@ -115,226 +138,269 @@ def tile_picked_ytop1_top1_p_kernel(tc, x_words, x_scales, w1, e_words, e_scales
         xg0 = sbuf([P, S], U32, "xg0")
         gather(xg0, xw[0], offs_sb, 0, S)
         wq = [quantize_w1(0, 1, "xw0")]
+        for i in range(TILES):
+            hidden_pass(i, 0, xg0[:, P * i : P * (i + 1)])
         round_w1(1, H // (2 * PACK))
         round_w1(2, SCALAR_SHARE)
         wq.append(quantize_w1(1, 2))
         xg1_first = sbuf([P, P], U32, "xg1_first")
         gather(xg1_first, xw[1], offs_sb, 0, P)
+        hidden_pass(0, 1, xg1_first[:])
         xg1_rest = sbuf([P, S - P], U32, "xg1_rest")
         gather(xg1_rest, xw[1], offs_sb, P, S - P)
-        eg = [sbuf([P, BANK], U32, "eg0")]
-        gather(eg[0], ew, neg_sb, 0, BANK)
+        for i in range(1, TILES):
+            hidden_pass(i, 1, xg1_rest[:, P * (i - 1) : P * i])
+        eg0 = sbuf([P, BANK], U32, "eg0")
+        gather(eg0, ew, neg_sb, 0, BANK)
+        eg = [[eg0[:]], []]
 
-        def hidden(i):
-            tok = slice(P * i, P * (i + 1))
-            x_codes = [xg0[:, tok], xg1_first[:] if i == 0 else xg1_rest[:, P * (i - 1) : P * i]]
-            h_ps = bank([P, PACK, P], H_BANKS[i], "h_ps")
-            for j in range(PACK):
-                for g in range(PASSES):
-                    nc.tensor.matmul_mx(
-                        out=h_ps[:, j, :],
-                        lhsT=wq[g][:, P * j : P * (j + 1)].bitcast(FP8X4),
-                        lhsT_scale=wsc[g][:, P * j : P * (j + 1)],
-                        rhs=x_codes[g].bitcast(FP8X4),
-                        rhs_scale=xsg[4 * g : P, tok],
-                        start=(g == 0),
-                        stop=(g == PASSES - 1),
-                    )
-            h_bf = sbuf([P, P * PACK], BF16, "h_bf%d" % i)
-            nc.scalar.activation(h_bf[:].rearrange("p (n j) -> p n j", j=PACK), h_ps[:].rearrange("p j n -> p n j"), ACT.Copy)
-            hq = sbuf([P, P], U32, "hq%d" % i)
-            hs = sbuf([P, P], U8, "hs%d" % i)
-            nc.vector.quantize_mx(out=hq[:].bitcast(FP8X4), scales=hs[:], in_=h_bf[:])
-            return hq, hs
+        h_bf = [sbuf([P, P * PACK], BF16, "h_bf%d" % i) for i in range(TILES)]
+        hq = [sbuf([P, P], U32, "hq%d" % i) for i in range(TILES)]
+        hs = [sbuf([P, P], U8, "hs%d" % i) for i in range(TILES)]
+
+        def round_h(i):
+            nc.scalar.activation(h_bf[i][:].rearrange("p (n j) -> p n j", j=PACK), h_ps[i][:].rearrange("p j n -> p n j"), ACT.Copy)
+
+        def quantize_h(i):
+            nc.vector.quantize_mx(out=hq[i][:].bitcast(FP8X4), scales=hs[i][:], in_=h_bf[i][:])
 
         y = {}
 
-        def scores(i, h):
-            hq, hs = quantised[i]
-            y[i, h] = bank([P, BANK], Y_BANKS[i][h], "y_ps")
-            nc.tensor.matmul_mx(
-                out=y[i, h][:], lhsT=hq[:].bitcast(FP8X4), lhsT_scale=hs[:],
-                rhs=eg[h][:].bitcast(FP8X4), rhs_scale=esg[h][:], start=True, stop=True,
-            )
+        def scores(u, b):
+            i, h = 2 * (u % 2) + b, u // 2
+            y[u, b] = bank([P, BANK], Y_BANKS[u][b], "y%d%d" % (u, b))
+            first = 0
+            for piece in eg[h]:
+                n = piece.shape[1]
+                nc.tensor.matmul_mx(
+                    out=y[u, b][:, first : first + n], lhsT=hq[i][:].bitcast(FP8X4), lhsT_scale=hs[i][:],
+                    rhs=piece.bitcast(FP8X4), rhs_scale=esg[h][E_PLANE:P, first : first + n], start=True, stop=True,
+                )
+                first = first + n
 
-        def add_turned(acc, terms, members):
-            for d in members:
-                nc.tensor.matmul(acc, lhsT=terms[:, d, :], rhs=ident[:], is_transpose=True, start=(d == 0), stop=(d == D - 1))
+        def add_turned(acc, terms, members=None, count=D):
+            for n, d in members or enumerate(range(count)):
+                nc.tensor.matmul(acc, lhsT=terms[:, d, :], rhs=ident[:], is_transpose=True, start=(n == 0), stop=(n == count - 1))
 
-        halves = [slice(GROUPS * h, GROUPS * (h + 1)) for h in range(U // BANK)]
-        member_halves = [slice(D // 2 * c, D // 2 * (c + 1)) for c in range(2)]
-        wide = [P, D, GROUPS]
-        args = [sbuf([P, 2 * D, V], F32, "args%d" % i) for i in range(TILES)]
-        th = [sbuf([P, 2 * D, V], F32, "th%d" % i) for i in range(TILES)]
-        ex = [sbuf([P, D, V], F32, "ex%d" % i) for i in range(TILES)]
-        z = [sbuf([P, D, V], F32, "z%d" % i) for i in range(TILES)]
-        top = [sbuf([P, V], F32, "top%d" % i) for i in range(TILES - 1)]
-        below = [sbuf([P, D, V], F32, "below%d" % i) for i in range(TILES - 1)]
-        both = [sbuf([P, D, V], F32, "both%d" % i) for i in range(TILES - 1)]
+        cols = [slice(GROUPS * b, GROUPS * (b + 1)) for b in range(2)]
+        whole = slice(0, P)
+        diff = [sbuf([P, D, P], F32, "diff%d" % u) for u in range(UNITS)]
+        sq = [sbuf([P, D, P], F32, "sq%d" % u) for u in range(UNITS)]
+        g1 = [sbuf([P, D, P], F32, "g1_%d" % u) for u in range(UNITS)]
+        g2 = [sbuf([P, D, P], F32, "g2_%d" % u) for u in range(UNITS)]
+        ex = [sbuf([P, D, P], F32, "ex%d" % u) for u in range(UNITS)]
+        z = [sbuf([P, D, P], F32, "z%d" % u) for u in range(UNITS)]
+        bounds = [sbuf([P, 2, P], F32, "bounds%d" % u) for u in range(UNITS)]
+        shift = [sbuf([P, P], F32, "shift%d" % u) for u in range(UNITS)]
 
-        def by_member(i, h):
-            return y[i, h][:].rearrange("p (v d) -> p d v", d=D)
+        def by_member(u, b):
+            return y[u, b][:].rearrange("p (v d) -> p d v", d=D)
 
-        def over_members(per_group):
-            return per_group.unsqueeze(1).to_broadcast(wide)
+        def largest(u, b):
+            nc.vector.tensor_reduce(bounds[u][:, 0, cols[b]], y[u, b][:].rearrange("p (v d) -> p v d", d=D), AXIS_X, ALU.max)
 
-        def largest(dst, i, h):
-            nc.vector.tensor_reduce(dst, y[i, h][:].rearrange("p (v d) -> p v d", d=D), mybir.AxisListType.X, ALU.max)
+        def upper(u, c):
+            if u < 2:
+                nc.vector.scalar_tensor_tensor(bounds[u][:, 1, c], bounds[u][:, 0, c], REACH, pos_flat(u)[:, c], ALU.add, ALU.min)
+            else:
+                nc.vector.scalar_tensor_tensor(bounds[u][:, 1, c], bounds[u][:, 0, c], 2 * REACH, raised[:, u - 2, c], ALU.add, ALU.min)
 
-        def minus_pos(i, h):
-            nc.vector.tensor_tensor(args[i][:, :D, halves[h]], by_member(i, h), over_members(pos_sb[:, i, halves[h]]), ALU.subtract)
+        def lower(u, c):
+            if u < 2:
+                nc.vector.scalar_tensor_tensor(shift[u][:, c], bounds[u][:, 0, c], -REACH, bounds[u][:, 1, c], ALU.add, ALU.max)
+            else:
+                nc.vector.tensor_reduce(shift[u][:, c], bounds[u][:, :, c].rearrange("p r v -> p v r"), AXIS_X, ALU.max)
 
-        def minus_top(i, h):
-            largest(top[i][:, halves[h]], i, h)
-            nc.vector.tensor_tensor(below[i][:, :, halves[h]], by_member(i, h), over_members(top[i][:, halves[h]]), ALU.subtract)
+        def subtract(u, b):
+            wide = shift[u][:, cols[b]].unsqueeze(1).to_broadcast([P, D, GROUPS])
+            nc.vector.scalar_tensor_tensor(diff[u][:, :, cols[b]], by_member(u, b), 0.0 if u < 2 else REACH, wide, ALU.add, ALU.subtract)
 
-        def squares(i, h):
-            nc.scalar.activation(args[i][:, D:, halves[h]], by_member(i, h), ACT.Square)
+        def fold(u):
+            folded = sbuf([P, D // 2, P], F32, "folded%d" % u)
+            nc.gpsimd.tensor_tensor(folded[:], g1[u][:, : D // 2, :], g1[u][:, D // 2 :, :], ALU.add)
+            return folded
 
-        def exps(i, h):
-            nc.scalar.activation(ex[i][:, :, halves[h]], below[i][:, :, halves[h]], ACT.Exp)
+        def squares(u, b):
+            nc.scalar.activation(sq[u][:, :, cols[b]], by_member(u, b), ACT.Square)
 
-        def gates(i, h):
-            nc.scalar.activation(th[i][:, :, halves[h]], args[i][:, :, halves[h]], ACT.Tanh, scale=0.5)
+        def gate2(u, c, members=slice(0, D)):
+            nc.scalar.activation(g2[u][:, members, c], sq[u][:, members, c], ACT.Sigmoid)
 
-        def add_gates(engine, i, h):
-            engine.tensor_tensor(both[i][:, :, halves[h]], th[i][:, :D, halves[h]], th[i][:, D:, halves[h]], ALU.add)
+        def gate1(u, c):
+            nc.scalar.activation(g1[u][:, :, c], diff[u][:, :, c], ACT.Sigmoid)
 
-        def weigh(i, h):
-            nc.gpsimd.tensor_tensor(z[i][:, :, halves[h]], both[i][:, :, halves[h]], ex[i][:, :, halves[h]], ALU.mult)
+        def weights(u, c):
+            nc.scalar.activation(ex[u][:, :, c], diff[u][:, :, c], ACT.Sigmoid, bias=minus_tail[:])
 
-        quantised = [hidden(0)]
+        def pos_flat(u):
+            return pos_sb[u // 2][:, 2 * (u % 2) : 2 * (u % 2) + 2, :].rearrange("p a v -> p (a v)")
+
+        def gather_e(first, name, takes_over):
+            piece = sbuf([P, BANK // 2], U32, name, takes_over)
+            gather(piece, ew, neg_sb, first, BANK // 2)
+            eg[1].append(piece[:])
+
+        def weigh_on(engine, u, members):
+            engine.tensor_tensor(z[u][:, members, :], g2[u][:, members, :], ex[u][:, members, :], ALU.mult)
+
+        halves = [slice(0, D // 2), slice(D // 2, D)]
+
+        def turn_back(dst, parts, start=0, stop=2):
+            for k in range(start, stop):
+                nc.tensor.matmul(dst, lhsT=parts[:, k, :], rhs=ident[:], is_transpose=True, start=(k == 0), stop=(k == 1))
+
+        round_h(0)
+        quantize_h(0)
         scores(0, 0)
-        eg.append(sbuf([P, BANK], U32, "eg1", "h_bf0"))
-        gather(eg[1], ew, neg_sb, BANK, BANK)
-        squares(0, 0)
-        minus_pos(0, 0)
-        quantised.extend(hidden(i) for i in range(1, TILES))
+        round_h(1)
+        quantize_h(1)
         scores(0, 1)
-        gates(0, 0)
-        add_gates(nc.gpsimd, 0, 0)
-        for i in (1, 2):
-            for h in range(2):
-                scores(i, h)
+        gather_e(BANK, "eg1a", "h_bf0")
+        round_h(2)
+        round_h(3)
+        largest(0, 0)
+        quantize_h(2)
         squares(0, 1)
-        minus_top(0, 0)
-        exps(0, 0)
-        weigh(0, 0)
+        upper(0, cols[0])
+        quantize_h(3)
+        squares(0, 0)
+        lower(0, cols[0])
+        largest(0, 1)
+        scores(1, 0)
+        scores(1, 1)
+        subtract(0, 0)
+        upper(0, cols[1])
+        gate2(0, whole)
+        pos_turned = bank([P, 2, P], 4, "pos_turned")
+        for u in (2, 3):
+            nc.tensor.transpose(pos_turned[:, u - 2, :], pos_flat(u), ident[:])
+        largest(1, 0)
+        lower(0, cols[1])
+        weights(0, cols[0])
+        gate1(0, cols[0])
+        largest(1, 1)
+        subtract(0, 1)
+        squares(1, 0)
+        upper(1, whole)
+        gather_e(BANK + BANK // 2, "eg1b", "bounds0")
+        lower(1, whole)
+        weights(0, cols[1])
+        pos_turned_sb = sbuf([P, 2, P], F32, "pos_turned_sb")
+        nc.scalar.activation(pos_turned_sb[:], pos_turned[:], ACT.Copy, bias=REACH)
+        squares(1, 1)
+        gate1(0, cols[1])
+        for members in halves:
+            weigh_on(nc.gpsimd, 0, members)
+        for u in (2, 3):
+            for b in range(2):
+                scores(u, b)
+        raised = bank([P, 2, P], 4, "raised")
+        for u in (2, 3):
+            nc.tensor.transpose(raised[:, u - 2, :], pos_turned_sb[:, u - 2, :], ident[:])
+        totals01 = bank([P, 2, P], 5, "totals01")
+        add_turned(totals01[:, 0, :], ex[0])
 
-        pos_turned = bank([P, P], 1, "pos_turned")
-        nc.tensor.transpose(pos_turned[:], pos_sb[:, 3, :], ident[:])
-        pos_turned_sb = sbuf([P, P], F32, "pos_turned_sb")
-        nc.scalar.activation(pos_turned_sb[:], pos_turned[:], ACT.Identity, bias=reach[:])
-        raised = bank([P, P], 1, "raised")
-        nc.tensor.transpose(raised[:], pos_turned_sb[:], ident[:])
-
-        for (i, h), ahead in (((0, 1), (1, 0)), ((1, 0), (1, 1)), ((1, 1), (2, 0))):
-            minus_pos(i, h)
-            squares(*ahead)
-            minus_top(i, h)
-            gates(i, h)
-            add_gates(nc.gpsimd, i, h)
-            exps(i, h)
-            weigh(i, h)
-            if i == 0:
-                scores(3, 0)
-                scores(3, 1)
-                totals01 = bank([P, 2, P], 0, "totals01")
-                add_turned(totals01[:, 0, :], ex[0], range(D))
-
-        bounds = sbuf([P, 2, V], F32, "bounds")
-        shift = sbuf([P, V], F32, "shift")
-        for h in range(2):
-            largest(bounds[:, 0, halves[h]], 3, h)
-        nc.vector.scalar_tensor_tensor(bounds[:, 1, :], bounds[:, 0, :], 2 * REACH, raised[:], ALU.add, ALU.min)
-        nc.vector.tensor_reduce(shift[:], bounds[:].rearrange("p r v -> p v r"), mybir.AxisListType.X, ALU.max)
-        for h in range(2):
-            nc.vector.scalar_tensor_tensor(args[3][:, :D, halves[h]], by_member(3, h), REACH, over_members(shift[:, halves[h]]), ALU.add, ALU.subtract)
-        minus_pos(2, 0)
-        add_turned(totals01[:, 1, :], ex[1], range(D))
-        gates(2, 0)
-        add_gates(nc.gpsimd, 2, 0)
+        subtract(1, 0)
+        largest(2, 0)
+        subtract(1, 1)
+        gate2(1, whole)
+        largest(2, 1)
+        gates01 = bank([P, 2, P], 6, "gates01")
+        add_turned(gates01[:, 1, :], g1[0])
+        upper(2, whole)
+        largest(3, 0)
+        lower(2, whole)
+        weights(1, whole)
+        squares(2, 0)
         squares(2, 1)
-        squares(3, 0)
-        squares(3, 1)
-        for c, members in enumerate(member_halves):
-            turned = bank([P, D // 2, P], 4 + c, "turned")
-            for d in range(D // 2):
-                nc.tensor.transpose(turned[:, d, :], args[3][:, members.start + d, :], ident[:])
-            nc.scalar.activation(ex[3][:, members, :], turned[:], ACT.Exp)
-
-        minus_pos(2, 1)
-        gates(2, 1)
-        minus_top(2, 0)
-        minus_top(2, 1)
-        totals23 = bank([P, 2, P], 6, "totals23")
-        add_turned(totals23[:, 0, :], ex[3], range(D))
-
+        nums01 = bank([P, 2, P], 7, "nums01")
+        add_turned(nums01[:, 1, :], z[0])
+        for members in halves:
+            weigh_on(nc.gpsimd, 1, members)
+        add_turned(totals01[:, 1, :], ex[1])
+        largest(3, 1)
+        subtract(2, 0)
+        upper(3, whole)
+        subtract(2, 1)
+        lower(3, whole)
+        gate1(1, whole)
+        folded1 = fold(1)
         total0 = sbuf([P, P], F32, "total0")
         nc.vector.tensor_copy(total0[:], totals01[:, 0, :])
-        prod01 = sbuf([P, P], F32, "prod01")
-        nc.vector.tensor_tensor(prod01[:], totals01[:, 1, :], total0[:], ALU.mult)
-        inv_prod01 = sbuf([P, P], F32, "inv_prod01")
-        nc.vector.reciprocal(inv_prod01[:], prod01[:])
-        total3 = sbuf([P, P], F32, "total3")
-        nc.vector.tensor_copy(total3[:], totals23[:, 0, :])
+        subtract(3, 0)
+        prod = sbuf([P, P], F32, "prod")
+        nc.vector.scalar_tensor_tensor(prod[:], totals01[:, 1, :], LIFT, total0[:], ALU.mult, ALU.mult)
+        subtract(3, 1)
+        weights(2, whole)
+        add_turned(nums01[:, 0, :], z[1])
+        total2 = bank([P, P], 4, "total2")
+        add_turned(total2[:], ex[2])
+        gate2(2, whole, halves[0])
+        weigh_on(nc.gpsimd, 2, halves[0])
+        add_turned(gates01[:, 0, :], folded1, count=D // 2)
+        inv_prod = sbuf([P, P], F32, "inv_prod")
+        nc.vector.reciprocal(inv_prod[:], prod[:])
+        weights(3, whole)
+        total3 = bank([P, P], 1, "total3")
+        add_turned(total3[:], ex[3])
+        gate2(2, whole, halves[1])
+        weigh_on(nc.gpsimd, 2, halves[1])
+        num2 = bank([P, P], 0, "num2")
+        add_turned(num2[:], z[2], [(d, d) for d in range(4)])
         inv10 = sbuf([P, 2, P], F32, "inv10")
-        nc.vector.tensor_tensor(inv10[:], totals01[:], inv_prod01[:].unsqueeze(1).to_broadcast([P, 2, P]), ALU.mult)
-
-        add_gates(nc.vector, 2, 1)
-        for members in member_halves:
-            nc.scalar.activation(ex[2][:, members, :], below[2][:, members, :], ACT.Exp)
-        nc.vector.scalar_tensor_tensor(z[2][:], both[2][:], 2.0, ex[2][:], ALU.add, ALU.mult)
-        add_turned(totals23[:, 1, :], ex[2], range(D))
-
-        ratios = []
-        for i, number in ((0, 1), (1, 7)):
-            num = bank([P, P], number, "num")
-            add_turned(num[:], z[i], range(D))
-            ratios.append(sbuf([P, P], F32, "ratio%d" % i))
-            nc.vector.tensor_tensor(ratios[i][:], num[:], inv10[:, 1 - i, :], ALU.mult)
-        back = bank([P, 2, P], 1, "back")
-        for i in range(2):
-            nc.tensor.transpose(back[:, i, :], ratios[i][:], ident[:])
-        prod23 = sbuf([P, P], F32, "prod23")
-        nc.vector.tensor_tensor(prod23[:], totals23[:, 1, :], total3[:], ALU.mult)
-        inv_prod23 = sbuf([P, P], F32, "inv_prod23")
-        nc.vector.reciprocal(inv_prod23[:], prod23[:])
-        inv2_turned = sbuf([P, P], F32, "inv2_turned")
-        nc.vector.tensor_tensor(inv2_turned[:], totals23[:, 0, :], inv_prod23[:], ALU.mult)
-
-        n = D // LAST_PIECES
-        pieces = [slice(n * c, n * (c + 1)) for c in range(LAST_PIECES)]
-        args3 = args[3][:].rearrange("p (k d) v -> p k d v", k=2)
-        th3 = th[3][:].rearrange("p (k d) v -> p k d v", k=2)
-        gate_sums = []
-        for members, number in zip(pieces, (4, 5, 2, 3)):
-            nc.scalar.activation(th3[:, :, members, :], args3[:, :, members, :], ACT.Tanh, scale=0.5)
-            gate_sums.append(bank([P, n, P], number, "gate_sums"))
-            for d in range(n):
-                for k in range(2):
-                    nc.tensor.matmul(gate_sums[-1][:, d, :], lhsT=th3[:, k, members.start + d, :], rhs=ident[:], is_transpose=True, start=(k == 0), stop=(k == 1))
-        res01 = sbuf([P, 2, V], F32, "res01")
-        nc.scalar.activation(res01[:], back[:], ACT.Copy, bias=1.0, scale=0.5)
-        nc.sync.dma_start(out[: 2 * P, :].rearrange("(a p) v -> p a v", p=P), res01[:])
-        fours = sbuf([P, D // 2, V], F32, "fours")
-        nc.gpsimd.tensor_tensor(fours[:], z[2][:, : D // 2, :], z[2][:, D // 2 :, :], ALU.add)
-        num3 = bank([P, P], 0, "num3")
-        for members, sums in zip(pieces, gate_sums):
-            nc.vector.scalar_tensor_tensor(z[3][:, members, :], sums[:], 2.0, ex[3][:, members, :], ALU.add, ALU.mult)
-            add_turned(num3[:], z[3], range(members.start, members.stop))
-
-        inv2 = bank([P, P], 4, "inv2")
-        nc.tensor.transpose(inv2[:], inv2_turned[:], ident[:])
-        twos = sbuf([P, 2, V], F32, "twos")
-        nc.gpsimd.tensor_tensor(twos[:], fours[:, :2, :], fours[:, 2:, :], ALU.add)
-        num2 = sbuf([P, V], F32, "num2")
-        nc.gpsimd.tensor_tensor(num2[:], twos[:, 0, :], twos[:, 1, :], ALU.add)
-        res2 = sbuf([P, V], F32, "res2")
-        nc.vector.scalar_tensor_tensor(res2[:], inv2[:], 0.5, num2[:], ALU.mult, ALU.mult)
-        nc.sync.dma_start(out[2 * P : 3 * P, :], res2[:])
-        inv3 = sbuf([P, P], F32, "inv3")
-        nc.vector.tensor_tensor(inv3[:], totals23[:, 1, :], inv_prod23[:], ALU.mult)
-        res3 = sbuf([P, V], F32, "res3")
-        nc.vector.scalar_tensor_tensor(res3[:], num3[:], 0.5, inv3[:], ALU.mult, ALU.mult)
-        nc.sync.dma_start(out[3 * P :, :], res3[:])
+        nc.vector.scalar_tensor_tensor(inv10[:], totals01[:], LIFT, inv_prod[:].unsqueeze(1).to_broadcast([P, 2, P]), ALU.mult, ALU.mult)
+        inv2 = sbuf([P, P], F32, "inv2")
+        nc.vector.reciprocal(inv2[:], total2[:])
+        gate1(2, whole)
+        folded2 = fold(2)
+        squares(3, 0)
+        parts01 = sbuf([P, 2, 2, P], F32, "parts01")
+        nc.vector.scalar_tensor_tensor(parts01[:, :, 0, :], gates01[:], minus_tiny[:], inv10[:], ALU.mult, ALU.mult)
+        nc.vector.tensor_tensor(parts01[:, :, 1, :], nums01[:], inv10[:], ALU.mult)
+        back01 = bank([P, 2, P], 5, "back01")
+        for u in range(2):
+            turn_back(back01[:, u, :], parts01[:, 1 - u])
+        add_turned(num2[:], z[2], [(d, d) for d in range(4, 8)])
+        turned3 = sbuf([P, 3, P], F32, "turned3")
+        nc.vector.reciprocal(turned3[:, 0, :], total3[:])
+        squares(3, 1)
+        gate2(3, cols[0])
+        gates2 = bank([P, P], 4, "gates2")
+        add_turned(gates2[:], folded2, count=D // 2)
+        terms = sbuf([P, D, P], F32, "terms")
+        nc.vector.tensor_copy(turned3[:, 1, :], total3[:])
+        parts2 = sbuf([P, 2, P], F32, "parts2")
+        nc.vector.tensor_tensor(terms[:, :, cols[0]], g2[3][:, :, cols[0]], ex[3][:, :, cols[0]], ALU.mult)
+        nc.vector.tensor_tensor(parts2[:, 1, :], num2[:], inv2[:], ALU.mult)
+        fours = sbuf([P, D // 2, P], F32, "fours")
+        nc.vector.tensor_tensor(fours[:, :, cols[0]], terms[:, halves[0], cols[0]], terms[:, halves[1], cols[0]], ALU.add)
+        nc.vector.scalar_tensor_tensor(parts2[:, 0, :], gates2[:], minus_tiny[:], inv2[:], ALU.mult, ALU.mult)
+        gates3 = bank([P, P], 6, "gates3")
+        for members in halves:
+            nc.scalar.activation(g1[3][:, members, :], diff[3][:, members, :], ACT.Sigmoid)
+            add_turned(gates3[:], g1[3], [(d, d) for d in range(members.start, members.stop)])
+        back2 = bank([P, P], 1, "back2")
+        turn_back(back2[:], parts2)
+        back3 = bank([P, 2, P], 7, "back3")
+        nc.tensor.transpose(back3[:, 0, :], turned3[:, 0, :], ident[:])
+        sums3 = sbuf([P, P], F32, "sums3")
+        nc.vector.tensor_reduce(sums3[:, cols[0]], fours[:, :, cols[0]].rearrange("p d v -> p v d"), AXIS_X, ALU.add)
+        quarters = [slice(GROUPS + 32 * c, GROUPS + 32 * (c + 1)) for c in range(2)]
+        for c in quarters:
+            gate2(3, c)
+            nc.vector.tensor_tensor(terms[:, :, c], g2[3][:, :, c], ex[3][:, :, c], ALU.mult)
+        nc.vector.scalar_tensor_tensor(turned3[:, 2, :], gates3[:], minus_tiny[:], turned3[:, 1, :], ALU.mult, ALU.add)
+        nc.tensor.transpose(back3[:, 1, :], turned3[:, 2, :], ident[:])
+        nc.vector.tensor_tensor(fours[:, :, cols[1]], terms[:, halves[0], cols[1]], terms[:, halves[1], cols[1]], ALU.add)
+        res01 = sbuf([P, 2, P], F32, "res01", "sq3")
+        nc.scalar.activation(res01[:], back01[:], ACT.Copy, bias=1.0)
+        nc.sync.dma_start(out[:, :GROUPS].rearrange("(a p) v -> p a v", p=P), res01[:].rearrange("p u (b v) -> p (u b) v", b=2))
+        nc.vector.tensor_reduce(sums3[:, cols[1]], fours[:, :, cols[1]].rearrange("p d v -> p v d"), AXIS_X, ALU.add)
+        res2 = sbuf([P, P], F32, "res2")
+        nc.scalar.activation(res2[:], back2[:], ACT.Copy, bias=1.0)
+        nc.sync.dma_start(out[: 2 * P, GROUPS:].rearrange("(a p) v -> p a v", p=P), res2[:].rearrange("p (b v) -> p b v", b=2))
+        whole3 = sbuf([P, P], F32, "whole3")
+        nc.vector.tensor_tensor(whole3[:], back3[:, 1, :], sums3[:], ALU.add)
+        res3 = sbuf([P, P], F32, "res3")
+        nc.vector.tensor_tensor(res3[:], back3[:, 0, :], whole3[:], ALU.mult)
+        nc.sync.dma_start(out[2 * P :, GROUPS:].rearrange("(a p) v -> p a v", p=P), res3[:].rearrange("p (b v) -> p b v", b=2))

@@ -32,7 +32,7 @@ LIFT = 2.0 ** 52
 E_PLANE = 8
 LAST_PIECES = 4
 H_BANKS = (0, 1, 2, 3)
-Y_BANKS = ((4, 5), (6, 7), (0, 1), (2, 3))
+Y_BANKS = ((4, 5), (6, 7), (0, 1), (2, 4))
 
 
 def tile_picked_ytop1_top1_p_kernel(tc, x_words, x_scales, w1, e_words, e_scales, pos, offs, neg, out):
@@ -235,9 +235,9 @@ def tile_picked_ytop1_top1_p_kernel(tc, x_words, x_scales, w1, e_words, e_scales
         def pos_flat(u):
             return pos_sb[u // 2][:, 2 * (u % 2) : 2 * (u % 2) + 2, :].rearrange("p a v -> p (a v)")
 
-        def gather_e(first, name, takes_over):
-            piece = sbuf([P, BANK // 2], U32, name, takes_over)
-            gather(piece, ew, neg_sb, first, BANK // 2)
+        def gather_e(first, count, takes_over):
+            piece = sbuf([P, count], U32, "eg1_%d" % first, takes_over)
+            gather(piece, ew, neg_sb, BANK + first, count)
             eg[1].append(piece[:])
 
         def weigh_on(engine, u, members):
@@ -252,66 +252,66 @@ def tile_picked_ytop1_top1_p_kernel(tc, x_words, x_scales, w1, e_words, e_scales
         round_h(0)
         quantize_h(0)
         scores(0, 0)
+        gather_e(0, P, "h_bf0")
         round_h(1)
         quantize_h(1)
         scores(0, 1)
-        gather_e(BANK, "eg1a", "h_bf0")
         round_h(2)
         round_h(3)
         largest(0, 0)
         quantize_h(2)
-        squares(0, 1)
         upper(0, cols[0])
-        quantize_h(3)
-        squares(0, 0)
-        lower(0, cols[0])
-        largest(0, 1)
-        scores(1, 0)
-        scores(1, 1)
-        subtract(0, 0)
-        upper(0, cols[1])
-        gate2(0, whole)
-        pos_turned = bank([P, 2, P], 4, "pos_turned")
+        pos_turned = bank([P, 2, P], 3, "pos_turned")
         for u in (2, 3):
             nc.tensor.transpose(pos_turned[:, u - 2, :], pos_flat(u), ident[:])
-        largest(1, 0)
-        lower(0, cols[1])
-        weights(0, cols[0])
-        gate1(0, cols[0])
-        largest(1, 1)
-        subtract(0, 1)
-        squares(1, 0)
-        upper(1, whole)
-        gather_e(BANK + BANK // 2, "eg1b", "bounds0")
-        lower(1, whole)
-        weights(0, cols[1])
+        scores(1, 0)
+        squares(0, 0)
+        largest(0, 1)
+        lower(0, cols[0])
+        quantize_h(3)
+        scores(1, 1)
         pos_turned_sb = sbuf([P, 2, P], F32, "pos_turned_sb")
         nc.scalar.activation(pos_turned_sb[:], pos_turned[:], ACT.Copy, bias=REACH)
+        upper(0, cols[1])
+        squares(0, 1)
+        subtract(0, 0)
+        lower(0, cols[1])
+        gate2(0, cols[0])
+        raised = bank([P, 2, P], 3, "raised")
+        for u in (2, 3):
+            nc.tensor.transpose(raised[:, u - 2, :], pos_turned_sb[:, u - 2, :], ident[:])
+        largest(1, 0)
+        weights(0, cols[0])
+        subtract(0, 1)
+        gate2(0, cols[1])
+        largest(1, 1)
+        gate1(0, cols[0])
+        squares(1, 0)
+        gather_e(P, 2 * P, "bounds0")
+        upper(1, whole)
+        gather_e(3 * P, P, "shift0")
+        lower(1, whole)
         squares(1, 1)
+        weights(0, cols[1])
         gate1(0, cols[1])
         for members in halves:
             weigh_on(nc.gpsimd, 0, members)
         for u in (2, 3):
             for b in range(2):
                 scores(u, b)
-        raised = bank([P, 2, P], 4, "raised")
-        for u in (2, 3):
-            nc.tensor.transpose(raised[:, u - 2, :], pos_turned_sb[:, u - 2, :], ident[:])
         totals01 = bank([P, 2, P], 5, "totals01")
         add_turned(totals01[:, 0, :], ex[0])
 
         subtract(1, 0)
-        largest(2, 0)
         subtract(1, 1)
+        largest(2, 0)
         gate2(1, whole)
         largest(2, 1)
         gates01 = bank([P, 2, P], 6, "gates01")
         add_turned(gates01[:, 1, :], g1[0])
-        upper(2, whole)
         largest(3, 0)
-        lower(2, whole)
+        upper(2, whole)
         weights(1, whole)
-        squares(2, 0)
         squares(2, 1)
         nums01 = bank([P, 2, P], 7, "nums01")
         add_turned(nums01[:, 1, :], z[0])
@@ -319,12 +319,14 @@ def tile_picked_ytop1_top1_p_kernel(tc, x_words, x_scales, w1, e_words, e_scales
             weigh_on(nc.gpsimd, 1, members)
         add_turned(totals01[:, 1, :], ex[1])
         largest(3, 1)
-        subtract(2, 0)
+        lower(2, whole)
         upper(3, whole)
+        subtract(2, 0)
         subtract(2, 1)
         lower(3, whole)
         gate1(1, whole)
         folded1 = fold(1)
+        squares(2, 0)
         total0 = sbuf([P, P], F32, "total0")
         nc.vector.tensor_copy(total0[:], totals01[:, 0, :])
         subtract(3, 0)
@@ -333,7 +335,7 @@ def tile_picked_ytop1_top1_p_kernel(tc, x_words, x_scales, w1, e_words, e_scales
         subtract(3, 1)
         weights(2, whole)
         add_turned(nums01[:, 0, :], z[1])
-        total2 = bank([P, P], 4, "total2")
+        total2 = bank([P, P], 3, "total2")
         add_turned(total2[:], ex[2])
         gate2(2, whole, halves[0])
         weigh_on(nc.gpsimd, 2, halves[0])
@@ -361,46 +363,47 @@ def tile_picked_ytop1_top1_p_kernel(tc, x_words, x_scales, w1, e_words, e_scales
         for u in range(2):
             turn_back(back01[:, u, :], parts01[:, 1 - u])
         add_turned(num2[:], z[2], [(d, d) for d in range(4, 8)])
-        turned3 = sbuf([P, 3, P], F32, "turned3")
+        turned3 = sbuf([P, 2, P], F32, "turned3")
         nc.vector.reciprocal(turned3[:, 0, :], total3[:])
         squares(3, 1)
         gate2(3, cols[0])
-        gates2 = bank([P, P], 4, "gates2")
+        gates2 = bank([P, P], 3, "gates2")
         add_turned(gates2[:], folded2, count=D // 2)
         terms = sbuf([P, D, P], F32, "terms")
-        nc.vector.tensor_copy(turned3[:, 1, :], total3[:])
         parts2 = sbuf([P, 2, P], F32, "parts2")
         nc.vector.tensor_tensor(terms[:, :, cols[0]], g2[3][:, :, cols[0]], ex[3][:, :, cols[0]], ALU.mult)
         nc.vector.tensor_tensor(parts2[:, 1, :], num2[:], inv2[:], ALU.mult)
         fours = sbuf([P, D // 2, P], F32, "fours")
         nc.vector.tensor_tensor(fours[:, :, cols[0]], terms[:, halves[0], cols[0]], terms[:, halves[1], cols[0]], ALU.add)
         nc.vector.scalar_tensor_tensor(parts2[:, 0, :], gates2[:], minus_tiny[:], inv2[:], ALU.mult, ALU.mult)
+        quarters = [slice(GROUPS + 32 * c, GROUPS + 32 * (c + 1)) for c in range(2)]
         gates3 = bank([P, P], 6, "gates3")
-        for members in halves:
+        for members, c in zip(halves, quarters):
             nc.scalar.activation(g1[3][:, members, :], diff[3][:, members, :], ACT.Sigmoid)
             add_turned(gates3[:], g1[3], [(d, d) for d in range(members.start, members.stop)])
+            gate2(3, c)
+        inv3 = bank([P, P], 7, "inv3")
+        nc.tensor.transpose(inv3[:], turned3[:, 0, :], ident[:])
         back2 = bank([P, P], 1, "back2")
         turn_back(back2[:], parts2)
-        back3 = bank([P, 2, P], 7, "back3")
-        nc.tensor.transpose(back3[:, 0, :], turned3[:, 0, :], ident[:])
         sums3 = sbuf([P, P], F32, "sums3")
+        nc.vector.tensor_tensor(terms[:, :, quarters[0]], g2[3][:, :, quarters[0]], ex[3][:, :, quarters[0]], ALU.mult)
         nc.vector.tensor_reduce(sums3[:, cols[0]], fours[:, :, cols[0]].rearrange("p d v -> p v d"), AXIS_X, ALU.add)
-        quarters = [slice(GROUPS + 32 * c, GROUPS + 32 * (c + 1)) for c in range(2)]
-        for c in quarters:
-            gate2(3, c)
-            nc.vector.tensor_tensor(terms[:, :, c], g2[3][:, :, c], ex[3][:, :, c], ALU.mult)
-        nc.vector.scalar_tensor_tensor(turned3[:, 2, :], gates3[:], minus_tiny[:], turned3[:, 1, :], ALU.mult, ALU.add)
-        nc.tensor.transpose(back3[:, 1, :], turned3[:, 2, :], ident[:])
-        nc.vector.tensor_tensor(fours[:, :, cols[1]], terms[:, halves[0], cols[1]], terms[:, halves[1], cols[1]], ALU.add)
+        nc.vector.tensor_tensor(fours[:, :, quarters[0]], terms[:, halves[0], quarters[0]], terms[:, halves[1], quarters[0]], ALU.add)
+        nc.vector.tensor_tensor(terms[:, :, quarters[1]], g2[3][:, :, quarters[1]], ex[3][:, :, quarters[1]], ALU.mult)
+        nc.vector.tensor_reduce(sums3[:, quarters[0]], fours[:, :, quarters[0]].rearrange("p d v -> p v d"), AXIS_X, ALU.add)
+        nc.vector.scalar_tensor_tensor(turned3[:, 1, :], gates3[:], minus_tiny[:], turned3[:, 0, :], ALU.mult, ALU.mult)
+        rest3 = bank([P, P], 2, "rest3")
+        nc.tensor.transpose(rest3[:], turned3[:, 1, :], ident[:])
+        nc.vector.tensor_reduce(sums3[:, quarters[1]], terms[:, :, quarters[1]].rearrange("p d v -> p v d"), AXIS_X, ALU.add)
         res01 = sbuf([P, 2, P], F32, "res01", "sq3")
         nc.scalar.activation(res01[:], back01[:], ACT.Copy, bias=1.0)
         nc.sync.dma_start(out[:, :GROUPS].rearrange("(a p) v -> p a v", p=P), res01[:].rearrange("p u (b v) -> p (u b) v", b=2))
-        nc.vector.tensor_reduce(sums3[:, cols[1]], fours[:, :, cols[1]].rearrange("p d v -> p v d"), AXIS_X, ALU.add)
         res2 = sbuf([P, P], F32, "res2")
         nc.scalar.activation(res2[:], back2[:], ACT.Copy, bias=1.0)
         nc.sync.dma_start(out[: 2 * P, GROUPS:].rearrange("(a p) v -> p a v", p=P), res2[:].rearrange("p (b v) -> p b v", b=2))
-        whole3 = sbuf([P, P], F32, "whole3")
-        nc.vector.tensor_tensor(whole3[:], back3[:, 1, :], sums3[:], ALU.add)
+        share3 = sbuf([P, P], F32, "share3")
+        nc.vector.tensor_tensor(share3[:], inv3[:], sums3[:], ALU.mult)
         res3 = sbuf([P, P], F32, "res3")
-        nc.vector.tensor_tensor(res3[:], back3[:, 0, :], whole3[:], ALU.mult)
+        nc.vector.scalar_tensor_tensor(res3[:], rest3[:], 1.0, share3[:], ALU.add, ALU.add)
         nc.sync.dma_start(out[2 * P :, GROUPS:].rearrange("(a p) v -> p a v", p=P), res3[:].rearrange("p (b v) -> p b v", b=2))

import math
from contextlib import ExitStack

import concourse.mybir as mybir
from concourse.masks import make_identity

K, T, S, H, D, V, W, U = 1024, 1024, 512, 512, 8, 128, 1024, 1024
FLOPS = 2 * K * H * S + 2 * H * S * U

F32 = mybir.dt.float32
BF16 = mybir.dt.bfloat16
I32 = mybir.dt.int32
U32 = mybir.dt.uint32
U16 = mybir.dt.uint16
U8 = mybir.dt.uint8
FP8X4 = mybir.dt.float8_e4m3fn_x4
ALU = mybir.AluOpType
ACT = mybir.ActivationFunctionType
AXIS_X = mybir.AxisListType.X

P = 128
PACK = 4
PASSES = K // (P * PACK)
BANK = 512
GROUPS = BANK // D
TILES = S // P
UNITS = 4
SCALAR_SHARE = 16
REACH = 18.0
TAIL = 36.0
LIFT = 2.0 ** 52
E_PLANE = 8
LAST_PIECES = 4
H_BANKS = (0, 1, 2, 3)
Y_BANKS = ((4, 5), (6, 7), (0, 1), (2, 4))


def tile_picked_ytop1_top1_p_kernel(tc, x_words, x_scales, w1, e_words, e_scales, pos, offs, neg, out):
    nc = tc.nc
    with ExitStack() as ctx:
        keep = ctx.enter_context(tc.tile_pool(name="keep", bufs=1))
        psum = ctx.enter_context(tc.psum_pool(name="psum", bufs=1))

        def sbuf(shape, dtype, name, takes_over=None):
            return keep.tile(shape, dtype, name=name, tag=takes_over or name, align_bytes=64)

        def bank(shape, number, name):
            return psum.tile(shape, F32, name=name, tag="bank%d" % number)

        offs_sb = keep.tile([P, S // 16], U16, name="offs_sb")
        neg_sb = keep.tile([P, U // 16], U16, name="neg_sb")
        xw = [sbuf([P, T], U32, "xw%d" % g) for g in range(PASSES)]
        xs = sbuf([P, T], U8, "xs")
        ew = sbuf([P, W], U32, "ew")
        es = sbuf([P, W], U8, "es")
        w_pieces = ((0, 0, H), (1, 0, H // 2), (1, H // 2, H // 2))
        w_raw = [sbuf([P, PACK, n], F32, "w_raw%d" % c) for c, (g, first, n) in enumerate(w_pieces)]
        pos_sb = [sbuf([P, TILES, GROUPS], F32, "pos_sb%d" % h) for h in range(2)]
        ident = sbuf([P, P], F32, "ident")

        nc.gpsimd.memset(es[:].bitcast(I32), 0)
        nc.gpsimd.memset(xs[:].bitcast(I32), 0)

        def load_words(dst, words):
            nc.sync.dma_start(dst[:].bitcast(I32), words.rearrange("p n t -> p (n t)").bitcast(I32))

        def load_w1(c, rows=slice(0, PACK)):
            g, first, n = w_pieces[c]
            src = w1[512 * g : 512 * (g + 1), first : first + n].rearrange("(p j) c -> p j c", j=PACK)
            nc.sync.dma_start(w_raw[c][:, rows, :], src[:, rows, :])

        nc.sync.dma_start(offs_sb[:], offs)
        nc.sync.dma_start(neg_sb[:], neg)
        load_w1(0, slice(0, 1))
        for q in range(4):
            nc.sync.dma_start(es[32 * q + E_PLANE : 32 * q + E_PLANE + 4, :].bitcast(I32), e_scales[0, 4 * q : 4 * q + 4, :].bitcast(I32))
        load_w1(0, slice(1, PACK))
        for q in range(4):
            nc.sync.dma_start(xs[32 * q : 32 * q + 4 * PASSES, :].bitcast(I32), x_scales[:, 4 * q : 4 * q + 4, :].bitcast(I32))
        load_words(xw[0], x_words[0])
        load_w1(1)
        load_w1(2)
        load_words(xw[1], x_words[1])
        load_words(ew, e_words[0])
        for h in range(2):
            nc.sync.dma_start(pos_sb[h][:], pos[:, GROUPS * h : GROUPS * (h + 1)].rearrange("(a p) v -> p a v", p=P))

        make_identity(nc, ident[:])
        minus_tail = sbuf([P, 1], F32, "minus_tail")
        nc.vector.memset(minus_tail[:], -TAIL)
        tiny = sbuf([P, 1], F32, "tiny")
        nc.scalar.activation(tiny[:], minus_tail[:], ACT.Sigmoid)
        minus_tiny = sbuf([P, 1], F32, "minus_tiny")
        nc.vector.tensor_scalar(minus_tiny[:], tiny[:], -1.0, None, ALU.mult)

        def gather(dst, table, places, first, count):
            nc.vector.tensor_copy(dst[:], table[:].indirect(places[:, first // 16 : (first + count) // 16]))

        w_bf = [sbuf([P, PACK * H], BF16, "w_bf%d" % g, earlier) for g, earlier in enumerate(("tiny", None))]
        wsc = [sbuf([P, H], U8, "wsc%d" % g) for g in range(PASSES)]

        def round_w1(c, on_scalar):
            g, first, n = w_pieces[c]
            dst = w_bf[g][:].rearrange("p (t m j) -> p m t j", t=PACK, j=PACK)[:, first // PACK : (first + n) // PACK]
            src = w_raw[c][:].rearrange("p j (m t) -> p m t j", t=PACK)
            nc.scalar.activation(dst[:, :on_scalar], src[:, :on_scalar], ACT.Copy)
            if on_scalar < n // PACK:
                nc.vector.tensor_copy(dst[:, on_scalar:], src[:, on_scalar:])

        def quantize_w1(g, pieces, takes_over=None):
            codes = sbuf([P, H], U32, "wq%d" % g, takes_over)
            n = H // pieces
            for c in range(pieces):
                cols = slice(n * c, n * (c + 1))
                nc.vector.quantize_mx(out=codes[:, cols].bitcast(FP8X4), scales=wsc[g][:, cols], in_=w_bf[g][:, PACK * n * c : PACK * n * (c + 1)])
            return codes

        h_ps = [bank([P, PACK, P], H_BANKS[i], "h_ps%d" % i) for i in range(TILES)]

        def hidden_pass(i, g, x_codes):
            for j in range(PACK):
                nc.tensor.matmul_mx(
                    out=h_ps[i][:, j, :],
                    lhsT=wq[g][:, P * j : P * (j + 1)].bitcast(FP8X4),
                    lhsT_scale=wsc[g][:, P * j : P * (j + 1)],
                    rhs=x_codes.bitcast(FP8X4),
                    rhs_scale=xsg[4 * g : P, P * i : P * (i + 1)],
                    start=(g == 0 and j == 0),
                    stop=(g == PASSES - 1 and j == PACK - 1),
                )

        esg = [sbuf([P, BANK], U8, "esg%d" % h) for h in range(2)]
        for h in range(2):
            gather(esg[h], es, neg_sb, BANK * h, BANK)
        round_w1(0, H // PACK)
        xsg = sbuf([P, S], U8, "xsg")
        gather(xsg, xs, offs_sb, 0, S)
        xg0 = sbuf([P, S], U32, "xg0")
        gather(xg0, xw[0], offs_sb, 0, S)
        wq = [quantize_w1(0, 1, "xw0")]
        for i in range(TILES):
            hidden_pass(i, 0, xg0[:, P * i : P * (i + 1)])
        round_w1(1, H // (2 * PACK))
        round_w1(2, SCALAR_SHARE)
        wq.append(quantize_w1(1, 2))
        xg1_first = sbuf([P, P], U32, "xg1_first")
        gather(xg1_first, xw[1], offs_sb, 0, P)
        hidden_pass(0, 1, xg1_first[:])
        xg1_rest = sbuf([P, S - P], U32, "xg1_rest")
        gather(xg1_rest, xw[1], offs_sb, P, S - P)
        for i in range(1, TILES):
            hidden_pass(i, 1, xg1_rest[:, P * (i - 1) : P * i])
        eg0 = sbuf([P, BANK], U32, "eg0")
        gather(eg0, ew, neg_sb, 0, BANK)
        eg = [[eg0[:]], []]

        h_bf = [sbuf([P, P * PACK], BF16, "h_bf%d" % i) for i in range(TILES)]
        hq = [sbuf([P, P], U32, "hq%d" % i) for i in range(TILES)]
        hs = [sbuf([P, P], U8, "hs%d" % i) for i in range(TILES)]

        def round_h(i):
            nc.scalar.activation(h_bf[i][:].rearrange("p (n j) -> p n j", j=PACK), h_ps[i][:].rearrange("p j n -> p n j"), ACT.Copy)

        def quantize_h(i):
            nc.vector.quantize_mx(out=hq[i][:].bitcast(FP8X4), scales=hs[i][:], in_=h_bf[i][:])

        y = {}

        def scores(u, b):
            i, h = 2 * (u % 2) + b, u // 2
            y[u, b] = bank([P, BANK], Y_BANKS[u][b], "y%d%d" % (u, b))
            first = 0
            for piece in eg[h]:
                n = piece.shape[1]
                nc.tensor.matmul_mx(
                    out=y[u, b][:, first : first + n], lhsT=hq[i][:].bitcast(FP8X4), lhsT_scale=hs[i][:],
                    rhs=piece.bitcast(FP8X4), rhs_scale=esg[h][E_PLANE:P, first : first + n], start=True, stop=True,
                )
                first = first + n

        def add_turned(acc, terms, members=None, count=D):
            for n, d in members or enumerate(range(count)):
                nc.tensor.matmul(acc, lhsT=terms[:, d, :], rhs=ident[:], is_transpose=True, start=(n == 0), stop=(n == count - 1))

        cols = [slice(GROUPS * b, GROUPS * (b + 1)) for b in range(2)]
        whole = slice(0, P)
        diff = [sbuf([P, D, P], F32, "diff%d" % u) for u in range(UNITS)]
        sq = [sbuf([P, D, P], F32, "sq%d" % u) for u in range(UNITS)]
        g1 = [sbuf([P, D, P], F32, "g1_%d" % u) for u in range(UNITS)]
        g2 = [sbuf([P, D, P], F32, "g2_%d" % u) for u in range(UNITS)]
        ex = [sbuf([P, D, P], F32, "ex%d" % u) for u in range(UNITS)]
        z = [sbuf([P, D, P], F32, "z%d" % u) for u in range(UNITS)]
        bounds = [sbuf([P, 2, P], F32, "bounds%d" % u) for u in range(UNITS)]
        shift = [sbuf([P, P], F32, "shift%d" % u) for u in range(UNITS)]

        def by_member(u, b):
            return y[u, b][:].rearrange("p (v d) -> p d v", d=D)

        def largest(u, b):
            nc.vector.tensor_reduce(bounds[u][:, 0, cols[b]], y[u, b][:].rearrange("p (v d) -> p v d", d=D), AXIS_X, ALU.max)

        def upper(u, c):
            if u < 2:
                nc.vector.scalar_tensor_tensor(bounds[u][:, 1, c], bounds[u][:, 0, c], REACH, pos_flat(u)[:, c], ALU.add, ALU.min)
            else:
                nc.vector.scalar_tensor_tensor(bounds[u][:, 1, c], bounds[u][:, 0, c], 2 * REACH, raised[:, u - 2, c], ALU.add, ALU.min)

        def lower(u, c):
            if u < 2:
                nc.vector.scalar_tensor_tensor(shift[u][:, c], bounds[u][:, 0, c], -REACH, bounds[u][:, 1, c], ALU.add, ALU.max)
            else:
                nc.vector.tensor_reduce(shift[u][:, c], bounds[u][:, :, c].rearrange("p r v -> p v r"), AXIS_X, ALU.max)

        def subtract(u, b):
            wide = shift[u][:, cols[b]].unsqueeze(1).to_broadcast([P, D, GROUPS])
            nc.vector.scalar_tensor_tensor(diff[u][:, :, cols[b]], by_member(u, b), 0.0 if u < 2 else REACH, wide, ALU.add, ALU.subtract)

        def fold(u):
            folded = sbuf([P, D // 2, P], F32, "folded%d" % u)
            nc.gpsimd.tensor_tensor(folded[:], g1[u][:, : D // 2, :], g1[u][:, D // 2 :, :], ALU.add)
            return folded

        def squares(u, b):
            nc.scalar.activation(sq[u][:, :, cols[b]], by_member(u, b), ACT.Square)

        def gate2(u, c, members=slice(0, D)):
            nc.scalar.activation(g2[u][:, members, c], sq[u][:, members, c], ACT.Sigmoid)

        def gate1(u, c):
            nc.scalar.activation(g1[u][:, :, c], diff[u][:, :, c], ACT.Sigmoid)

        def weights(u, c):
            nc.scalar.activation(ex[u][:, :, c], diff[u][:, :, c], ACT.Sigmoid, bias=minus_tail[:])

        def pos_flat(u):
            return pos_sb[u // 2][:, 2 * (u % 2) : 2 * (u % 2) + 2, :].rearrange("p a v -> p (a v)")

        def gather_e(first, count, takes_over):
            piece = sbuf([P, count], U32, "eg1_%d" % first, takes_over)
            gather(piece, ew, neg_sb, BANK + first, count)
            eg[1].append(piece[:])

        def weigh_on(engine, u, members):
            engine.tensor_tensor(z[u][:, members, :], g2[u][:, members, :], ex[u][:, members, :], ALU.mult)

        halves = [slice(0, D // 2), slice(D // 2, D)]

        def turn_back(dst, parts, start=0, stop=2):
            for k in range(start, stop):
                nc.tensor.matmul(dst, lhsT=parts[:, k, :], rhs=ident[:], is_transpose=True, start=(k == 0), stop=(k == 1))

        round_h(0)
        quantize_h(0)
        scores(0, 0)
        gather_e(0, P, "h_bf0")
        round_h(1)
        quantize_h(1)
        scores(0, 1)
        round_h(2)
        round_h(3)
        largest(0, 0)
        quantize_h(2)
        upper(0, cols[0])
        pos_turned = bank([P, 2, P], 3, "pos_turned")
        for u in (2, 3):
            nc.tensor.transpose(pos_turned[:, u - 2, :], pos_flat(u), ident[:])
        scores(1, 0)
        squares(0, 0)
        largest(0, 1)
        lower(0, cols[0])
        quantize_h(3)
        scores(1, 1)
        pos_turned_sb = sbuf([P, 2, P], F32, "pos_turned_sb")
        nc.scalar.activation(pos_turned_sb[:], pos_turned[:], ACT.Copy, bias=REACH)
        upper(0, cols[1])
        squares(0, 1)
        subtract(0, 0)
        lower(0, cols[1])
        gate2(0, cols[0])
        raised = bank([P, 2, P], 3, "raised")
        for u in (2, 3):
            nc.tensor.transpose(raised[:, u - 2, :], pos_turned_sb[:, u - 2, :], ident[:])
        largest(1, 0)
        weights(0, cols[0])
        subtract(0, 1)
        gate2(0, cols[1])
        largest(1, 1)
        gate1(0, cols[0])
        squares(1, 0)
        gather_e(P, 2 * P, "bounds0")
        upper(1, whole)
        gather_e(3 * P, P, "shift0")
        lower(1, whole)
        squares(1, 1)
        weights(0, cols[1])
        gate1(0, cols[1])
        for members in halves:
            weigh_on(nc.gpsimd, 0, members)
        for u in (2, 3):
            for b in range(2):
                scores(u, b)
        totals01 = bank([P, 2, P], 5, "totals01")
        add_turned(totals01[:, 0, :], ex[0])

        subtract(1, 0)
        subtract(1, 1)
        largest(2, 0)
        gate2(1, whole)
        largest(2, 1)
        gates01 = bank([P, 2, P], 6, "gates01")
        add_turned(gates01[:, 1, :], g1[0])
        largest(3, 0)
        upper(2, whole)
        weights(1, whole)
        squares(2, 1)
        nums01 = bank([P, 2, P], 7, "nums01")
        add_turned(nums01[:, 1, :], z[0])
        for members in halves:
            weigh_on(nc.gpsimd, 1, members)
        add_turned(totals01[:, 1, :], ex[1])
        largest(3, 1)
        lower(2, whole)
        upper(3, whole)
        subtract(2, 0)
        subtract(2, 1)
        lower(3, whole)
        gate1(1, whole)
        folded1 = fold(1)
        squares(2, 0)
        total0 = sbuf([P, P], F32, "total0")
        nc.vector.tensor_copy(total0[:], totals01[:, 0, :])
        subtract(3, 0)
        prod = sbuf([P, P], F32, "prod")
        nc.vector.scalar_tensor_tensor(prod[:], totals01[:, 1, :], LIFT, total0[:], ALU.mult, ALU.mult)
        subtract(3, 1)
        weights(2, whole)
        add_turned(nums01[:, 0, :], z[1])
        total2 = bank([P, P], 3, "total2")
        add_turned(total2[:], ex[2])
        gate2(2, whole, halves[0])
        weigh_on(nc.gpsimd, 2, halves[0])
        add_turned(gates01[:, 0, :], folded1, count=D // 2)
        inv_prod = sbuf([P, P], F32, "inv_prod")
        nc.vector.reciprocal(inv_prod[:], prod[:])
        weights(3, whole)
        total3 = bank([P, P], 1, "total3")
        add_turned(total3[:], ex[3])
        gate2(2, whole, halves[1])
        weigh_on(nc.gpsimd, 2, halves[1])
        num2 = bank([P, P], 0, "num2")
        add_turned(num2[:], z[2], [(d, d) for d in range(4)])
        inv10 = sbuf([P, 2, P], F32, "inv10")
        nc.vector.scalar_tensor_tensor(inv10[:], totals01[:], LIFT, inv_prod[:].unsqueeze(1).to_broadcast([P, 2, P]), ALU.mult, ALU.mult)
        inv2 = sbuf([P, P], F32, "inv2")
        nc.vector.reciprocal(inv2[:], total2[:])
        gate1(2, whole)
        folded2 = fold(2)
        squares(3, 0)
        parts01 = sbuf([P, 2, 2, P], F32, "parts01")
        nc.vector.scalar_tensor_tensor(parts01[:, :, 0, :], gates01[:], minus_tiny[:], inv10[:], ALU.mult, ALU.mult)
        nc.vector.tensor_tensor(parts01[:, :, 1, :], nums01[:], inv10[:], ALU.mult)
        back01 = bank([P, 2, P], 5, "back01")
        for u in range(2):
            turn_back(back01[:, u, :], parts01[:, 1 - u])
        add_turned(num2[:], z[2], [(d, d) for d in range(4, 8)])
        turned3 = sbuf([P, 2, P], F32, "turned3")
        nc.vector.reciprocal(turned3[:, 0, :], total3[:])
        squares(3, 1)
        gate2(3, cols[0])
        gates2 = bank([P, P], 3, "gates2")
        add_turned(gates2[:], folded2, count=D // 2)
        terms = sbuf([P, D, P], F32, "terms")
        parts2 = sbuf([P, 2, P], F32, "parts2")
        nc.vector.tensor_tensor(terms[:, :, cols[0]], g2[3][:, :, cols[0]], ex[3][:, :, cols[0]], ALU.mult)
        nc.vector.tensor_tensor(parts2[:, 1, :], num2[:], inv2[:], ALU.mult)
        fours = sbuf([P, D // 2, P], F32, "fours")
        nc.vector.tensor_tensor(fours[:, :, cols[0]], terms[:, halves[0], cols[0]], terms[:, halves[1], cols[0]], ALU.add)
        nc.vector.scalar_tensor_tensor(parts2[:, 0, :], gates2[:], minus_tiny[:], inv2[:], ALU.mult, ALU.mult)
        quarters = [slice(GROUPS + 32 * c, GROUPS + 32 * (c + 1)) for c in range(2)]
        gates3 = bank([P, P], 6, "gates3")
        for members, c in zip(halves, quarters):
            nc.scalar.activation(g1[3][:, members, :], diff[3][:, members, :], ACT.Sigmoid)
            add_turned(gates3[:], g1[3], [(d, d) for d in range(members.start, members.stop)])
            gate2(3, c)
        inv3 = bank([P, P], 7, "inv3")
        nc.tensor.transpose(inv3[:], turned3[:, 0, :], ident[:])
        back2 = bank([P, P], 1, "back2")
        turn_back(back2[:], parts2)
        sums3 = sbuf([P, P], F32, "sums3")
        nc.vector.tensor_tensor(terms[:, :, quarters[0]], g2[3][:, :, quarters[0]], ex[3][:, :, quarters[0]], ALU.mult)
        nc.vector.tensor_reduce(sums3[:, cols[0]], fours[:, :, cols[0]].rearrange("p d v -> p v d"), AXIS_X, ALU.add)
        nc.vector.tensor_tensor(fours[:, :, quarters[0]], terms[:, halves[0], quarters[0]], terms[:, halves[1], quarters[0]], ALU.add)
        nc.vector.tensor_tensor(terms[:, :, quarters[1]], g2[3][:, :, quarters[1]], ex[3][:, :, quarters[1]], ALU.mult)
        nc.vector.tensor_reduce(sums3[:, quarters[0]], fours[:, :, quarters[0]].rearrange("p d v -> p v d"), AXIS_X, ALU.add)
        nc.vector.scalar_tensor_tensor(turned3[:, 1, :], gates3[:], minus_tiny[:], turned3[:, 0, :], ALU.mult, ALU.mult)
        rest3 = bank([P, P], 2, "rest3")
        nc.tensor.transpose(rest3[:], turned3[:, 1, :], ident[:])
        nc.vector.tensor_reduce(sums3[:, quarters[1]], terms[:, :, quarters[1]].rearrange("p d v -> p v d"), AXIS_X, ALU.add)
        res01 = sbuf([P, 2, P], F32, "res01", "sq3")
        nc.scalar.activation(res01[:], back01[:], ACT.Copy, bias=1.0)
        nc.sync.dma_start(out[:, :GROUPS].rearrange("(a p) v -> p a v", p=P), res01[:].rearrange("p u (b v) -> p (u b) v", b=2))
        res2 = sbuf([P, P], F32, "res2")
        nc.scalar.activation(res2[:], back2[:], ACT.Copy, bias=1.0)
        nc.sync.dma_start(out[: 2 * P, GROUPS:].rearrange("(a p) v -> p a v", p=P), res2[:].rearrange("p (b v) -> p b v", b=2))
        share3 = sbuf([P, P], F32, "share3")
        nc.vector.tensor_tensor(share3[:], inv3[:], sums3[:], ALU.mult)
        res3 = sbuf([P, P], F32, "res3")
        nc.vector.scalar_tensor_tensor(res3[:], rest3[:], 1.0, share3[:], ALU.add, ALU.add)
        nc.sync.dma_start(out[2 * P :, GROUPS:].rearrange("(a p) v -> p a v", p=P), res3[:].rearrange("p (b v) -> p b v", b=2))
